import numpy as np
import ml_dtypes


def mxq(x, axis, fmt="e4m3"):
    dtype, down = {"e4m3": (ml_dtypes.float8_e4m3fn, 7), "e5m2": (ml_dtypes.float8_e5m2, 14)}[fmt]
    v = np.moveaxis(np.asarray(x, np.float32).astype(ml_dtypes.bfloat16).astype(np.float64), axis, -1)
    blocks = v.reshape(v.shape[:-1] + (-1, 32))
    amax = np.abs(blocks).max(-1, keepdims=True)
    byte = np.maximum(np.where(amax > 0, np.frexp(amax)[1] - 1 + 127, 0) - down, 1)
    scale = np.exp2(byte - 127.0)
    codes = (blocks / scale).astype(np.float32).astype(dtype).astype(np.float64)
    return np.moveaxis((codes * scale).reshape(v.shape), -1, axis)


WIDE = False


def mx_kscale(k):
    if not WIDE:
        return np.ones(k)
    levels = np.array([10, -10, 5, -5, 0])
    if k % 512:
        return np.exp2(np.random.permutation(np.resize(levels, k // 32))).repeat(32)
    a = np.empty((k // 512, 16))
    for p in range(k // 512):
        a[p, :8] = np.random.permutation(np.resize(levels, 8))
        for g in range(8):
            far = levels[np.abs(levels - a[p, g]) >= 10]
            a[p, g + 8] = far[np.random.randint(len(far))]
    return np.exp2(a.ravel()).repeat(32)


def f64(x):
    return np.asarray(x).astype(np.float64)


def striped(idx):
    return np.tile(idx.reshape(-1, 16).T, (8, 1)).astype(np.uint16)


def unstriped(offs):
    return offs[:16].T.reshape(-1).astype(np.int64)


def striped8(idx):
    return np.concatenate([x.reshape(-1, 16).T for x in idx]).astype(np.uint16)


def runs(offs, k):
    lists = np.stack([offs[16 * r : 16 * r + 16].T.reshape(-1) for r in range(8)]).astype(np.int64)
    return lists[np.arange(k) % 512 // 64]


def pack_weight(w):
    k, n = w.shape
    w = f64(np.asarray(w, np.float32).astype(ml_dtypes.bfloat16)).reshape(k // 32, 32, n)
    amax = np.abs(w).max(1)
    byte = np.clip(np.where(amax > 0, np.frexp(amax)[1] - 1 + 127 - 7, 1), 1, 254)
    scaled = (w * np.exp2(127.0 - byte)[:, None, :]).reshape(k, n).astype(np.float32)
    words = np.ascontiguousarray(scaled.reshape(k // 512, 128, 4, n).transpose(0, 1, 3, 2)).astype(ml_dtypes.float8_e4m3fn).view(np.uint8)
    return words, np.ascontiguousarray(byte.astype(np.uint8).reshape(k // 512, 16, n))


def unpack_weight(words, scales):
    g, p, n, _ = words.shape
    vals = np.ascontiguousarray(words).view(ml_dtypes.float8_e4m3fn).astype(np.float64) * np.repeat(np.exp2(scales.astype(np.float64) - 127.0), 8, axis=1)[..., None]
    return vals.transpose(0, 1, 3, 2).reshape(g * 512, n)

def planes(y):
    n, m = y.shape
    v = y.astype(np.float32).astype(ml_dtypes.bfloat16).astype(np.float64).reshape(n // 32, 32, m)
    top = np.abs(v).max(1)
    byte = np.clip(np.where(top > 0, np.frexp(top)[1] - 1 + 127 - 7, 1), 1, 254)
    codes = (v * np.exp2(127.0 - byte)[:, None, :]).reshape(n, m).astype(np.float32).astype(ml_dtypes.float8_e4m3fn).view(np.uint8)
    words = codes.reshape(n // 512, 128, 4, m).transpose(0, 1, 3, 2)
    return np.ascontiguousarray(words), np.ascontiguousarray(byte.astype(np.uint8).reshape(n // 512, 16, m))


K, T, S, V, N, H = 512, 2048, 512, 256, 512, 512


def setup_inputs():
    n = np.random.standard_normal
    s = mx_kscale(K)[:, None]
    u = mx_kscale(H)
    packed_xT = pack_weight(n((K, T)) * s)
    packed_w2 = pack_weight(n((H, N)) / np.sqrt(H) / u[:, None])
    perm = np.stack([np.random.permutation(S) for _ in range(8)])
    return {
        "x_words": packed_xT[0],
        "x_scales": packed_xT[1],
        "w1": (n((K, H)) / np.sqrt(K) / s * u).astype(np.float32),
        "w2_words": packed_w2[0],
        "w2_scales": packed_w2[1],
        "offs": striped(np.random.permutation(T)[:S]),
        "la": striped8(perm[:, :V]),
        "lb": striped8(perm[:, V:]),
    }


def reference(x_words, x_scales, w1, w2_words, w2_scales, offs, la, lb):
    xq = unpack_weight(x_words, x_scales)[:, unstriped(offs)]
    y = mxq(f64(w1), 0, "e4m3").T @ xq
    a = y[np.arange(H)[:, None], runs(la, H)]
    b = y[np.arange(H)[:, None], runs(lb, H)]
    df = 0.75 * (a - b)
    sm = 0.75 * (a + b)
    p = np.zeros((H, S))
    p[np.arange(H)[:, None], runs(la, H)] = sm
    z = p.copy()
    z[np.arange(H)[:, None], runs(lb, H)] = df
    out_0 = unpack_weight(w2_words, w2_scales).T @ mxq(z, 0, "e4m3")
    return (out_0,) + planes(out_0)

@@ -1,0 +1,195 @@
+from contextlib import ExitStack
+
+import concourse.mybir as mybir
+
+K, T, S, V, N, H = 512, 2048, 512, 256, 512, 512
+
+F32 = mybir.dt.float32
+BF16 = mybir.dt.bfloat16
+I32 = mybir.dt.int32
+U32 = mybir.dt.uint32
+U16 = mybir.dt.uint16
+U8 = mybir.dt.uint8
+FP8X4 = mybir.dt.float8_e4m3fn_x4
+COPY = mybir.ActivationFunctionType.Copy
+ADD = mybir.AluOpType.add
+
+P = 128
+PACK = 4
+QUADS = 4
+HALF = S // 2
+CHUNK = 128
+CHUNKS = S // CHUNK
+LINE = 4
+
+FLOPS = 2 * K * H * S + 2 * H * N * S
+
+
+def load_scale_rows(queue, plane, rows):
+    for q in range(QUADS):
+        queue.dma_start(out=plane[32 * q : 32 * q + 4, :].bitcast(I32), in_=rows[4 * q : 4 * q + 4, :].bitcast(I32))
+
+
+def tile_picked_haarinp_none_po_kernel(tc, x_words, x_scales, w1, w2_words, w2_scales, offs, la, lb, out_0, out_1, out_2):
+    nc = tc.nc
+    with ExitStack() as ctx:
+        keep = ctx.enter_context(tc.tile_pool(name="keep", bufs=1))
+        psum = ctx.enter_context(tc.psum_pool(name="psum", bufs=8))
+
+        def tiles(name, count, shape, dtype):
+            return [keep.tile(shape, dtype, name="%s%d" % (name, i), align_bytes=64) for i in range(count)]
+
+        offs_sb = keep.tile([P, S // 16], U16, name="offs_sb")
+        la_sb = keep.tile([P, V // 16], U16, name="la_sb")
+        lb_sb = keep.tile([P, V // 16], U16, name="lb_sb")
+        x_word_table = keep.tile([P, T], U32, name="x_word_table", align_bytes=64)
+        x_scale_table = keep.tile([P, T], U8, name="x_scale_table", align_bytes=64)
+        w1_raw = keep.tile([P, PACK, H], F32, name="w1_raw", tag="weights_raw", align_bytes=64)
+        w2_scale_raw = keep.tile([P, N], U8, name="w2_scale_raw", align_bytes=64)
+
+        nc.vector.memset(x_scale_table[:].bitcast(I32), 0)
+        nc.gpsimd.memset(w2_scale_raw[:].bitcast(I32), 0)
+
+        nc.sync.dma_start(offs_sb[:], offs)
+        nc.sync.dma_start(out=w1_raw[:], in_=w1.rearrange("(p j) c -> p j c", j=PACK))
+        load_scale_rows(nc.scalar, x_scale_table, x_scales[0])
+        nc.sync.dma_start(out=x_word_table[:].bitcast(I32), in_=x_words[0].rearrange("p n t -> p (n t)").bitcast(I32))
+        nc.sync.dma_start(la_sb[:], la)
+        nc.sync.dma_start(lb_sb[:], lb)
+        load_scale_rows(nc.gpsimd, w2_scale_raw, w2_scales[0])
+
+        w1_grouped = [
+            keep.tile([P, 2, P, PACK], BF16, name="w1_grouped%d" % u, tag="w1_grouped%d" % u, align_bytes=64)
+            for u in range(2)
+        ]
+        w1_codes = tiles("w1_codes", 2, [P, 2 * P], U32)
+        w1_scale = tiles("w1_scale", 2, [P, 2 * P], U8)
+        w1_src = w1_raw[:].rearrange("p j (m t) -> p m j t", t=PACK)
+
+        def quantise_w1(u):
+            nc.vector.quantize_mx(
+                out=w1_codes[u][:].bitcast(FP8X4),
+                scales=w1_scale[u][:],
+                in_=w1_grouped[u][:].rearrange("p e m j -> p (e m j)"),
+            )
+
+        nc.vector.tensor_copy(out=w1_grouped[0][:].rearrange("p e m j -> p m j e"), in_=w1_src[:, :, :, 0:2])
+        nc.scalar.copy(out=w1_grouped[1][:].rearrange("p e m j -> p m j e"), in_=w1_src[:, :, :, 2:4])
+        w2_word_raw = keep.tile([P, N], U32, name="w2_word_raw", tag="weights_raw", align_bytes=64)
+        nc.sync.dma_start(out=w2_word_raw[:].bitcast(I32), in_=w2_words[0].rearrange("p n t -> p (n t)").bitcast(I32))
+        quantise_w1(0)
+        x_scale_picked = keep.tile([P, S], U8, name="x_scale_picked", tag="w1_grouped0", align_bytes=64)
+        nc.vector.tensor_copy(out=x_scale_picked[:], in_=x_scale_table[:].indirect(offs_sb[:]))
+        x_word_picked = tiles("x_word_picked", 2, [P, HALF], U32)
+        for h in range(2):
+            entries = offs_sb[:, h * (HALF // 16) : (h + 1) * (HALF // 16)]
+            nc.vector.tensor_copy(out=x_word_picked[h][:], in_=x_word_table[:].indirect(entries))
+        quantise_w1(1)
+
+        y = tiles("y", PACK, [P, S], F32)
+        for t in range(PACK):
+            for h in range(2):
+                cols = slice(h * HALF, (h + 1) * HALF)
+                acc = psum.tile([P, HALF], F32, name="acc", tag="bank")
+                nc.tensor.matmul_mx(
+                    out=acc[:],
+                    lhsT=w1_codes[t // 2][:, t % 2 * P : (t % 2 + 1) * P].bitcast(FP8X4),
+                    lhsT_scale=w1_scale[t // 2][:, t % 2 * P : (t % 2 + 1) * P],
+                    rhs=x_word_picked[h][:].bitcast(FP8X4),
+                    rhs_scale=x_scale_picked[:, cols],
+                    start=True,
+                    stop=True,
+                )
+                nc.scalar.activation(out=y[t][:, cols], in_=acc[:], func=COPY, scale=0.75)
+
+        w2_codes = keep.tile([P, N], U32, name="w2_codes", align_bytes=64)
+        w2_scale = keep.tile([P, N], U8, name="w2_scale", align_bytes=64)
+        nc.vector.tensor_copy(
+            out=w2_codes[:].bitcast(I32).rearrange("p (t m) -> p m t", t=PACK),
+            in_=w2_word_raw[:].bitcast(I32).rearrange("p (m t) -> p m t", t=PACK),
+        )
+        nc.vector.tensor_copy(
+            out=w2_scale[:].rearrange("p (t m) -> p m t", t=PACK),
+            in_=w2_scale_raw[:].rearrange("p (m t) -> p m t", t=PACK),
+        )
+
+        a = tiles("a", PACK, [P, V], F32)
+        b = tiles("b", PACK, [P, V], F32)
+        minus_b = tiles("minus_b", PACK, [P, V], F32)
+        z = tiles("z", PACK, [P, S], F32)
+        z_grouped = tiles("z_grouped", CHUNKS, [P, CHUNK, PACK], BF16)
+
+        def fetch_a(t):
+            nc.vector.tensor_copy(out=a[t][:], in_=y[t][:].indirect(la_sb[:]))
+
+        def fetch_b(t):
+            nc.vector.tensor_copy(out=b[t][:], in_=y[t][:].indirect(lb_sb[:]))
+            nc.scalar.activation(out=minus_b[t][:], in_=b[t][:], func=COPY, scale=-1.0)
+
+        def put_sum(t):
+            nc.vector.tensor_tensor(z[t][:].indirect(la_sb[:]), a[t][:], b[t][:], ADD)
+
+        def put_difference(t):
+            nc.vector.tensor_tensor(z[t][:].indirect(lb_sb[:]), a[t][:], minus_b[t][:], ADD)
+            for c in range(CHUNKS):
+                nc.scalar.copy(out=z_grouped[c][:, :, t], in_=z[t][:, c * CHUNK : (c + 1) * CHUNK])
+
+        fetch_b(0)
+        fetch_a(0)
+        for t in range(PACK):
+            if t + 1 < PACK:
+                fetch_b(t + 1)
+            put_sum(t)
+            if t + 1 < PACK:
+                fetch_a(t + 1)
+            put_difference(t)
+
+        z_codes = tiles("z_codes", CHUNKS, [P, CHUNK], U32)
+        z_scale = tiles("z_scale", CHUNKS, [P, CHUNK], U8)
+        result = tiles("result", CHUNKS, [P, PACK, CHUNK], F32)
+        result_grouped = tiles("result_grouped", CHUNKS, [P, CHUNK, PACK], BF16)
+        out_codes = keep.tile([P, S], U32, name="out_codes", align_bytes=64)
+        out_scale = keep.tile([P, S], U8, name="out_scale", align_bytes=64)
+        out_rows = out_0.rearrange("(p t) n -> p t n", t=PACK)
+        out_words = out_1[0].rearrange("p n t -> p (n t)").bitcast(I32)
+
+        for c in range(CHUNKS):
+            nc.vector.quantize_mx(
+                out=z_codes[c][:].bitcast(FP8X4),
+                scales=z_scale[c][:],
+                in_=z_grouped[c][:].rearrange("p n t -> p (n t)"),
+            )
+        for c in range(CHUNKS):
+            cols = slice(c * CHUNK, (c + 1) * CHUNK)
+            acc = psum.tile([P, PACK, CHUNK], F32, name="acc", tag="bank")
+            for t in range(PACK):
+                nc.tensor.matmul_mx(
+                    out=acc[:, t, :],
+                    lhsT=w2_codes[:, t * P : (t + 1) * P].bitcast(FP8X4),
+                    lhsT_scale=w2_scale[:, t * P : (t + 1) * P],
+                    rhs=z_codes[c][:].bitcast(FP8X4),
+                    rhs_scale=z_scale[c][:],
+                    start=True,
+                    stop=True,
+                )
+            nc.scalar.copy(out=result[c][:], in_=acc[:])
+            nc.sync.dma_start(out=out_rows[:, :, cols], in_=result[c][:])
+            nc.vector.tensor_copy(
+                out=result_grouped[c][:].rearrange("p (g i) t -> p g t i", i=LINE),
+                in_=result[c][:].rearrange("p t (g i) -> p g t i", i=LINE),
+            )
+            nc.vector.quantize_mx(
+                out=out_codes[:, cols].bitcast(FP8X4),
+                scales=out_scale[:, cols],
+                in_=result_grouped[c][:].rearrange("p n t -> p (n t)"),
+            )
+            if c == CHUNKS - 2:
+                nc.sync.dma_start(out=out_words[:, : (c + 1) * CHUNK], in_=out_codes[:, : (c + 1) * CHUNK].bitcast(I32))
+            if c == CHUNKS - 1:
+                nc.sync.dma_start(out=out_words[:, cols], in_=out_codes[:, cols].bitcast(I32))
+        for q in range(QUADS):
+            queue = nc.sync if q % 2 == 0 else nc.scalar
+            queue.dma_start(
+                out=out_2[0][4 * q : 4 * q + 4, :].bitcast(I32),
+                in_=out_scale[32 * q : 32 * q + 4, :].bitcast(I32),
+            )

@@ -45,18 +45,15 @@ def tile_picked_haarinp_none_po_kernel(tc, x_words, x_scales, w1, w2_words, w2_s
         x_word_table = keep.tile([P, T], U32, name="x_word_table", align_bytes=64)
         x_scale_table = keep.tile([P, T], U8, name="x_scale_table", align_bytes=64)
         w1_raw = keep.tile([P, PACK, H], F32, name="w1_raw", tag="weights_raw", align_bytes=64)
-        w2_scale_raw = keep.tile([P, N], U8, name="w2_scale_raw", align_bytes=64)
 
         nc.vector.memset(x_scale_table[:].bitcast(I32), 0)
-        nc.gpsimd.memset(w2_scale_raw[:].bitcast(I32), 0)
 
         nc.sync.dma_start(offs_sb[:], offs)
         nc.sync.dma_start(out=w1_raw[:], in_=w1.rearrange("(p j) c -> p j c", j=PACK))
-        load_scale_rows(nc.scalar, x_scale_table, x_scales[0])
+        load_scale_rows(nc.sync, x_scale_table, x_scales[0])
         nc.sync.dma_start(out=x_word_table[:].bitcast(I32), in_=x_words[0].rearrange("p n t -> p (n t)").bitcast(I32))
         nc.sync.dma_start(la_sb[:], la)
         nc.sync.dma_start(lb_sb[:], lb)
-        load_scale_rows(nc.gpsimd, w2_scale_raw, w2_scales[0])
 
         w1_grouped = [
             keep.tile([P, 2, P, PACK], BF16, name="w1_grouped%d" % u, tag="w1_grouped%d" % u, align_bytes=64)
@@ -80,22 +77,26 @@ def tile_picked_haarinp_none_po_kernel(tc, x_words, x_scales, w1, w2_words, w2_s
         quantise_w1(0)
         x_scale_picked = keep.tile([P, S], U8, name="x_scale_picked", tag="w1_grouped0", align_bytes=64)
         nc.vector.tensor_copy(out=x_scale_picked[:], in_=x_scale_table[:].indirect(offs_sb[:]))
-        x_word_picked = tiles("x_word_picked", 2, [P, HALF], U32)
+        x_word_picked = keep.tile([P, S], U32, name="x_word_picked", align_bytes=64)
         for h in range(2):
             entries = offs_sb[:, h * (HALF // 16) : (h + 1) * (HALF // 16)]
-            nc.vector.tensor_copy(out=x_word_picked[h][:], in_=x_word_table[:].indirect(entries))
+            nc.vector.tensor_copy(out=x_word_picked[:, h * HALF : (h + 1) * HALF], in_=x_word_table[:].indirect(entries))
         quantise_w1(1)
+        w2_scale_raw = keep.tile([P, N], U8, name="w2_scale_raw", tag="w1_grouped1", align_bytes=64)
+        nc.gpsimd.memset(w2_scale_raw[:].bitcast(I32), 0)
+        load_scale_rows(nc.sync, w2_scale_raw, w2_scales[0])
 
         y = tiles("y", PACK, [P, S], F32)
         for t in range(PACK):
-            for h in range(2):
-                cols = slice(h * HALF, (h + 1) * HALF)
-                acc = psum.tile([P, HALF], F32, name="acc", tag="bank")
+            width = HALF if t == 0 else S
+            for first in range(0, S, width):
+                cols = slice(first, first + width)
+                acc = psum.tile([P, width], F32, name="acc", tag="bank")
                 nc.tensor.matmul_mx(
                     out=acc[:],
                     lhsT=w1_codes[t // 2][:, t % 2 * P : (t % 2 + 1) * P].bitcast(FP8X4),
                     lhsT_scale=w1_scale[t // 2][:, t % 2 * P : (t % 2 + 1) * P],
-                    rhs=x_word_picked[h][:].bitcast(FP8X4),
+                    rhs=x_word_picked[:, cols].bitcast(FP8X4),
                     rhs_scale=x_scale_picked[:, cols],
                     start=True,
                     stop=True,
@@ -103,19 +104,16 @@ def tile_picked_haarinp_none_po_kernel(tc, x_words, x_scales, w1, w2_words, w2_s
                 nc.scalar.activation(out=y[t][:, cols], in_=acc[:], func=COPY, scale=0.75)
 
         w2_codes = keep.tile([P, N], U32, name="w2_codes", align_bytes=64)
-        w2_scale = keep.tile([P, N], U8, name="w2_scale", align_bytes=64)
         nc.vector.tensor_copy(
             out=w2_codes[:].bitcast(I32).rearrange("p (t m) -> p m t", t=PACK),
             in_=w2_word_raw[:].bitcast(I32).rearrange("p (m t) -> p m t", t=PACK),
         )
-        nc.vector.tensor_copy(
-            out=w2_scale[:].rearrange("p (t m) -> p m t", t=PACK),
-            in_=w2_scale_raw[:].rearrange("p (m t) -> p m t", t=PACK),
-        )
 
         a = tiles("a", PACK, [P, V], F32)
         b = tiles("b", PACK, [P, V], F32)
-        minus_b = tiles("minus_b", PACK, [P, V], F32)
+        minus_b = [
+            keep.tile([P, V], F32, name="minus_b%d" % t, tag="minus_b%d" % t, align_bytes=64) for t in range(PACK)
+        ]
         z = tiles("z", PACK, [P, S], F32)
         z_grouped = tiles("z_grouped", CHUNKS, [P, CHUNK, PACK], BF16)
 
@@ -144,6 +142,11 @@ def tile_picked_haarinp_none_po_kernel(tc, x_words, x_scales, w1, w2_words, w2_s
                 fetch_a(t + 1)
             put_difference(t)
 
+        w2_scale = keep.tile([P, N], U8, name="w2_scale", tag="minus_b%d" % (PACK - 1), align_bytes=64)
+        nc.vector.tensor_copy(
+            out=w2_scale[:].rearrange("p (t m) -> p m t", t=PACK),
+            in_=w2_scale_raw[:].rearrange("p (m t) -> p m t", t=PACK),
+        )
         z_codes = tiles("z_codes", CHUNKS, [P, CHUNK], U32)
         z_scale = tiles("z_scale", CHUNKS, [P, CHUNK], U8)
         result = tiles("result", CHUNKS, [P, PACK, CHUNK], F32)

@@ -21,6 +21,7 @@ HALF = S // 2
 CHUNK = 128
 CHUNKS = S // CHUNK
 LINE = 4
+PLANE_ORDER = (0, 2, 3, 1)
 
 FLOPS = 2 * K * H * S + 2 * H * N * S
 
@@ -44,58 +45,53 @@ def tile_picked_haarinp_none_po_kernel(tc, x_words, x_scales, w1, w2_words, w2_s
         lb_sb = keep.tile([P, V // 16], U16, name="lb_sb")
         x_word_table = keep.tile([P, T], U32, name="x_word_table", align_bytes=64)
         x_scale_table = keep.tile([P, T], U8, name="x_scale_table", align_bytes=64)
-        w1_raw = keep.tile([P, PACK, H], F32, name="w1_raw", tag="weights_raw", align_bytes=64)
+        w1_raw = tiles("w1_raw", 2, [P, PACK, H // 2], F32)
+        w2_word_raw = keep.tile([P, N], U32, name="w2_word_raw", align_bytes=64)
+        w2_scale_raw = keep.tile([P, N], U8, name="w2_scale_raw", align_bytes=64)
 
         nc.vector.memset(x_scale_table[:].bitcast(I32), 0)
+        nc.vector.memset(w2_scale_raw[:].bitcast(I32), 0)
 
+        w1_rows = w1.rearrange("(p j) c -> p j c", j=PACK)
         nc.sync.dma_start(offs_sb[:], offs)
-        nc.sync.dma_start(out=w1_raw[:], in_=w1.rearrange("(p j) c -> p j c", j=PACK))
-        load_scale_rows(nc.sync, x_scale_table, x_scales[0])
         nc.sync.dma_start(out=x_word_table[:].bitcast(I32), in_=x_words[0].rearrange("p n t -> p (n t)").bitcast(I32))
-        nc.sync.dma_start(la_sb[:], la)
-        nc.sync.dma_start(lb_sb[:], lb)
-
-        w1_grouped = [
-            keep.tile([P, 2, P, PACK], BF16, name="w1_grouped%d" % u, tag="w1_grouped%d" % u, align_bytes=64)
-            for u in range(2)
-        ]
-        w1_codes = tiles("w1_codes", 2, [P, 2 * P], U32)
-        w1_scale = tiles("w1_scale", 2, [P, 2 * P], U8)
-        w1_src = w1_raw[:].rearrange("p j (m t) -> p m j t", t=PACK)
-
-        def quantise_w1(u):
-            nc.vector.quantize_mx(
-                out=w1_codes[u][:].bitcast(FP8X4),
-                scales=w1_scale[u][:],
-                in_=w1_grouped[u][:].rearrange("p e m j -> p (e m j)"),
-            )
-
-        nc.vector.tensor_copy(out=w1_grouped[0][:].rearrange("p e m j -> p m j e"), in_=w1_src[:, :, :, 0:2])
-        nc.scalar.copy(out=w1_grouped[1][:].rearrange("p e m j -> p m j e"), in_=w1_src[:, :, :, 2:4])
-        w2_word_raw = keep.tile([P, N], U32, name="w2_word_raw", tag="weights_raw", align_bytes=64)
-        nc.sync.dma_start(out=w2_word_raw[:].bitcast(I32), in_=w2_words[0].rearrange("p n t -> p (n t)").bitcast(I32))
-        quantise_w1(0)
-        x_scale_picked = keep.tile([P, S], U8, name="x_scale_picked", tag="w1_grouped0", align_bytes=64)
-        nc.vector.tensor_copy(out=x_scale_picked[:], in_=x_scale_table[:].indirect(offs_sb[:]))
-        x_word_picked = keep.tile([P, S], U32, name="x_word_picked", align_bytes=64)
+        load_scale_rows(nc.sync, x_scale_table, x_scales[0])
         for h in range(2):
-            entries = offs_sb[:, h * (HALF // 16) : (h + 1) * (HALF // 16)]
-            nc.vector.tensor_copy(out=x_word_picked[:, h * HALF : (h + 1) * HALF], in_=x_word_table[:].indirect(entries))
-        quantise_w1(1)
-        w2_scale_raw = keep.tile([P, N], U8, name="w2_scale_raw", tag="w1_grouped1", align_bytes=64)
-        nc.gpsimd.memset(w2_scale_raw[:].bitcast(I32), 0)
+            nc.sync.dma_start(out=w1_raw[h][:], in_=w1_rows[:, :, h * (H // 2) : (h + 1) * (H // 2)])
+        nc.sync.dma_start(lb_sb[:], lb)
+        nc.sync.dma_start(la_sb[:], la)
+        nc.sync.dma_start(out=w2_word_raw[:].bitcast(I32), in_=w2_words[0].rearrange("p n t -> p (n t)").bitcast(I32))
         load_scale_rows(nc.sync, w2_scale_raw, w2_scales[0])
 
+        x_word_picked = keep.tile([P, S], U32, name="x_word_picked", align_bytes=64)
+        x_scale_picked = keep.tile([P, S], U8, name="x_scale_picked", align_bytes=64)
+        nc.vector.tensor_copy(out=x_word_picked[:], in_=x_word_table[:].indirect(offs_sb[:]))
+        nc.vector.tensor_copy(out=x_scale_picked[:], in_=x_scale_table[:].indirect(offs_sb[:]))
+
+        w1_grouped = tiles("w1_grouped", 2, [P, 2, P, PACK], BF16)
+        w1_codes = tiles("w1_codes", PACK, [P, P], U32)
+        w1_scale = tiles("w1_scale", PACK, [P, P], U8)
+        for h in range(2):
+            src = w1_raw[h][:].rearrange("p j (m e u) -> p u m j e", e=2, u=2)
+            ms = slice(h * (P // 2), (h + 1) * (P // 2))
+            nc.vector.tensor_copy(out=w1_grouped[0][:, :, ms, :].rearrange("p e m j -> p m j e"), in_=src[:, 0])
+            nc.scalar.copy(out=w1_grouped[1][:, :, ms, :].rearrange("p e m j -> p m j e"), in_=src[:, 1])
+
         y = tiles("y", PACK, [P, S], F32)
-        for t in range(PACK):
-            width = HALF if t == 0 else S
+        for t in PLANE_ORDER:
+            nc.vector.quantize_mx(
+                out=w1_codes[t][:].bitcast(FP8X4),
+                scales=w1_scale[t][:],
+                in_=w1_grouped[t % 2][:, t // 2].rearrange("p m j -> p (m j)"),
+            )
+            width = HALF if t == PLANE_ORDER[0] else S
             for first in range(0, S, width):
                 cols = slice(first, first + width)
                 acc = psum.tile([P, width], F32, name="acc", tag="bank")
                 nc.tensor.matmul_mx(
                     out=acc[:],
-                    lhsT=w1_codes[t // 2][:, t % 2 * P : (t % 2 + 1) * P].bitcast(FP8X4),
-                    lhsT_scale=w1_scale[t // 2][:, t % 2 * P : (t % 2 + 1) * P],
+                    lhsT=w1_codes[t][:].bitcast(FP8X4),
+                    lhsT_scale=w1_scale[t][:],
                     rhs=x_word_picked[:, cols].bitcast(FP8X4),
                     rhs_scale=x_scale_picked[:, cols],
                     start=True,
@@ -104,49 +100,41 @@ def tile_picked_haarinp_none_po_kernel(tc, x_words, x_scales, w1, w2_words, w2_s
                 nc.scalar.activation(out=y[t][:, cols], in_=acc[:], func=COPY, scale=0.75)
 
         w2_codes = keep.tile([P, N], U32, name="w2_codes", align_bytes=64)
+        w2_scale = keep.tile([P, N], U8, name="w2_scale", align_bytes=64)
         nc.vector.tensor_copy(
-            out=w2_codes[:].bitcast(I32).rearrange("p (t m) -> p m t", t=PACK),
-            in_=w2_word_raw[:].bitcast(I32).rearrange("p (m t) -> p m t", t=PACK),
+            out=w2_codes[:].bitcast(I32).rearrange("p (t g i) -> p g t i", t=PACK, i=4),
+            in_=w2_word_raw[:].bitcast(I32).rearrange("p (g i t) -> p g t i", t=PACK, i=4),
+        )
+        nc.vector.tensor_copy(
+            out=w2_scale[:].rearrange("p (t g i) -> p g t i", t=PACK, i=16),
+            in_=w2_scale_raw[:].rearrange("p (g i t) -> p g t i", t=PACK, i=16),
         )
 
         a = tiles("a", PACK, [P, V], F32)
         b = tiles("b", PACK, [P, V], F32)
-        minus_b = [
-            keep.tile([P, V], F32, name="minus_b%d" % t, tag="minus_b%d" % t, align_bytes=64) for t in range(PACK)
-        ]
-        z = tiles("z", PACK, [P, S], F32)
+        z = [keep.tile([P, S], F32, name="z%d" % t, tag="z%d" % t, align_bytes=64) for t in range(PACK)]
+        minus_b = {}
         z_grouped = tiles("z_grouped", CHUNKS, [P, CHUNK, PACK], BF16)
 
-        def fetch_a(t):
-            nc.vector.tensor_copy(out=a[t][:], in_=y[t][:].indirect(la_sb[:]))
+        for pair in (PLANE_ORDER[:2], PLANE_ORDER[2:]):
+            for t in pair:
+                nc.vector.tensor_copy(out=b[t][:], in_=y[t][:].indirect(lb_sb[:]))
+                tag = "z%d" % PLANE_ORDER[0] if t == PLANE_ORDER[-1] else "minus_b%d" % t
+                minus_b[t] = keep.tile([P, V], F32, name="minus_b%d" % t, tag=tag, align_bytes=64)
+                nc.scalar.activation(out=minus_b[t][:], in_=b[t][:], func=COPY, scale=-1.0)
+                nc.vector.tensor_copy(out=a[t][:], in_=y[t][:].indirect(la_sb[:]))
+            for t in pair:
+                nc.vector.tensor_tensor(z[t][:].indirect(la_sb[:]), a[t][:], b[t][:], ADD)
+            for t in pair:
+                nc.vector.tensor_tensor(z[t][:].indirect(lb_sb[:]), a[t][:], minus_b[t][:], ADD)
+                for c in range(CHUNKS):
+                    dst = z_grouped[c][:, :, t]
+                    src = z[t][:, c * CHUNK : (c + 1) * CHUNK]
+                    if t == PLANE_ORDER[-1] and c < CHUNKS // 2:
+                        nc.vector.tensor_copy(out=dst, in_=src)
+                    else:
+                        nc.scalar.copy(out=dst, in_=src)
 
-        def fetch_b(t):
-            nc.vector.tensor_copy(out=b[t][:], in_=y[t][:].indirect(lb_sb[:]))
-            nc.scalar.activation(out=minus_b[t][:], in_=b[t][:], func=COPY, scale=-1.0)
-
-        def put_sum(t):
-            nc.vector.tensor_tensor(z[t][:].indirect(la_sb[:]), a[t][:], b[t][:], ADD)
-
-        def put_difference(t):
-            nc.vector.tensor_tensor(z[t][:].indirect(lb_sb[:]), a[t][:], minus_b[t][:], ADD)
-            for c in range(CHUNKS):
-                nc.scalar.copy(out=z_grouped[c][:, :, t], in_=z[t][:, c * CHUNK : (c + 1) * CHUNK])
-
-        fetch_b(0)
-        fetch_a(0)
-        for t in range(PACK):
-            if t + 1 < PACK:
-                fetch_b(t + 1)
-            put_sum(t)
-            if t + 1 < PACK:
-                fetch_a(t + 1)
-            put_difference(t)
-
-        w2_scale = keep.tile([P, N], U8, name="w2_scale", tag="minus_b%d" % (PACK - 1), align_bytes=64)
-        nc.vector.tensor_copy(
-            out=w2_scale[:].rearrange("p (t m) -> p m t", t=PACK),
-            in_=w2_scale_raw[:].rearrange("p (m t) -> p m t", t=PACK),
-        )
         z_codes = tiles("z_codes", CHUNKS, [P, CHUNK], U32)
         z_scale = tiles("z_scale", CHUNKS, [P, CHUNK], U8)
         result = tiles("result", CHUNKS, [P, PACK, CHUNK], F32)

@@ -78,7 +78,12 @@ def tile_picked_haarinp_none_po_kernel(tc, x_words, x_scales, w1, w2_words, w2_s
             nc.scalar.copy(out=w1_grouped[1][:, :, ms, :].rearrange("p e m j -> p m j e"), in_=src[:, 1])
 
         y = tiles("y", PACK, [P, S], F32)
-        for t in PLANE_ORDER:
+        z = [keep.tile([P, S], F32, name="z%d" % t, tag="z%d" % t, align_bytes=64) for t in range(PACK)]
+        z_grouped = tiles("z_grouped", CHUNKS, [P, CHUNK, PACK], BF16)
+        w2_codes = keep.tile([P, N], U32, name="w2_codes", align_bytes=64)
+        w2_scale = keep.tile([P, N], U8, name="w2_scale", align_bytes=64)
+
+        def project(t):
             nc.vector.quantize_mx(
                 out=w1_codes[t][:].bitcast(FP8X4),
                 scales=w1_scale[t][:],
@@ -99,29 +104,25 @@ def tile_picked_haarinp_none_po_kernel(tc, x_words, x_scales, w1, w2_words, w2_s
                 )
                 nc.scalar.activation(out=y[t][:, cols], in_=acc[:], func=COPY, scale=0.75)
 
-        w2_codes = keep.tile([P, N], U32, name="w2_codes", align_bytes=64)
-        w2_scale = keep.tile([P, N], U8, name="w2_scale", align_bytes=64)
-        nc.vector.tensor_copy(
-            out=w2_codes[:].bitcast(I32).rearrange("p (t g i) -> p g t i", t=PACK, i=4),
-            in_=w2_word_raw[:].bitcast(I32).rearrange("p (g i t) -> p g t i", t=PACK, i=4),
-        )
-        nc.vector.tensor_copy(
-            out=w2_scale[:].rearrange("p (t g i) -> p g t i", t=PACK, i=16),
-            in_=w2_scale_raw[:].rearrange("p (g i t) -> p g t i", t=PACK, i=16),
-        )
+        def deal_w2():
+            nc.vector.tensor_copy(
+                out=w2_codes[:].bitcast(I32).rearrange("p (t g i) -> p g t i", t=PACK, i=4),
+                in_=w2_word_raw[:].bitcast(I32).rearrange("p (g i t) -> p g t i", t=PACK, i=4),
+            )
+            nc.vector.tensor_copy(
+                out=w2_scale[:].rearrange("p (t g i) -> p g t i", t=PACK, i=16),
+                in_=w2_scale_raw[:].rearrange("p (g i t) -> p g t i", t=PACK, i=16),
+            )
 
-        a = tiles("a", PACK, [P, V], F32)
-        b = tiles("b", PACK, [P, V], F32)
-        z = [keep.tile([P, S], F32, name="z%d" % t, tag="z%d" % t, align_bytes=64) for t in range(PACK)]
-        minus_b = {}
-        z_grouped = tiles("z_grouped", CHUNKS, [P, CHUNK, PACK], BF16)
-
-        for pair in (PLANE_ORDER[:2], PLANE_ORDER[2:]):
-            for t in pair:
+        def haar(pair):
+            a, b, minus_b = {}, {}, {}
+            for slot, t in enumerate(pair):
+                b[t] = keep.tile([P, V], F32, name="b%d" % t, tag="b%d" % slot, align_bytes=64)
                 nc.vector.tensor_copy(out=b[t][:], in_=y[t][:].indirect(lb_sb[:]))
                 tag = "z%d" % PLANE_ORDER[0] if t == PLANE_ORDER[-1] else "minus_b%d" % t
                 minus_b[t] = keep.tile([P, V], F32, name="minus_b%d" % t, tag=tag, align_bytes=64)
                 nc.scalar.activation(out=minus_b[t][:], in_=b[t][:], func=COPY, scale=-1.0)
+                a[t] = keep.tile([P, V], F32, name="a%d" % t, tag="a%d" % slot, align_bytes=64)
                 nc.vector.tensor_copy(out=a[t][:], in_=y[t][:].indirect(la_sb[:]))
             for t in pair:
                 nc.vector.tensor_tensor(z[t][:].indirect(la_sb[:]), a[t][:], b[t][:], ADD)
@@ -134,6 +135,14 @@ def tile_picked_haarinp_none_po_kernel(tc, x_words, x_scales, w1, w2_words, w2_s
                         nc.vector.tensor_copy(out=dst, in_=src)
                     else:
                         nc.scalar.copy(out=dst, in_=src)
+
+        for t in PLANE_ORDER[:2]:
+            project(t)
+        haar(PLANE_ORDER[:2])
+        for t in PLANE_ORDER[2:]:
+            project(t)
+        deal_w2()
+        haar(PLANE_ORDER[2:])
 
         z_codes = tiles("z_codes", CHUNKS, [P, CHUNK], U32)
         z_scale = tiles("z_scale", CHUNKS, [P, CHUNK], U8)
@@ -165,10 +174,13 @@ def tile_picked_haarinp_none_po_kernel(tc, x_words, x_scales, w1, w2_words, w2_s
                 )
             nc.scalar.copy(out=result[c][:], in_=acc[:])
             nc.sync.dma_start(out=out_rows[:, :, cols], in_=result[c][:])
-            nc.vector.tensor_copy(
-                out=result_grouped[c][:].rearrange("p (g i) t -> p g t i", i=LINE),
-                in_=result[c][:].rearrange("p t (g i) -> p g t i", i=LINE),
-            )
+            if c == CHUNKS - 1:
+                nc.scalar.copy(out=result_grouped[c][:], in_=acc[:].rearrange("p t n -> p n t"))
+            else:
+                nc.vector.tensor_copy(
+                    out=result_grouped[c][:].rearrange("p (g i) t -> p g t i", i=LINE),
+                    in_=result[c][:].rearrange("p t (g i) -> p g t i", i=LINE),
+                )
             nc.vector.quantize_mx(
                 out=out_codes[:, cols].bitcast(FP8X4),
                 scales=out_scale[:, cols],
@@ -177,7 +189,7 @@ def tile_picked_haarinp_none_po_kernel(tc, x_words, x_scales, w1, w2_words, w2_s
             if c == CHUNKS - 2:
                 nc.sync.dma_start(out=out_words[:, : (c + 1) * CHUNK], in_=out_codes[:, : (c + 1) * CHUNK].bitcast(I32))
             if c == CHUNKS - 1:
-                nc.sync.dma_start(out=out_words[:, cols], in_=out_codes[:, cols].bitcast(I32))
+                nc.scalar.dma_start(out=out_words[:, cols], in_=out_codes[:, cols].bitcast(I32))
         for q in range(QUADS):
             queue = nc.sync if q % 2 == 0 else nc.scalar
             queue.dma_start(

@@ -35,7 +35,8 @@ def tile_picked_haarinp_none_po_kernel(tc, x_words, x_scales, w1, w2_words, w2_s
     nc = tc.nc
     with ExitStack() as ctx:
         keep = ctx.enter_context(tc.tile_pool(name="keep", bufs=1))
-        psum = ctx.enter_context(tc.psum_pool(name="psum", bufs=8))
+        shared = ctx.enter_context(tc.tile_pool(name="shared", bufs=1))
+        psum = ctx.enter_context(tc.psum_pool(name="psum", bufs=7))
 
         def tiles(name, count, shape, dtype):
             return [keep.tile(shape, dtype, name="%s%d" % (name, i), align_bytes=64) for i in range(count)]
@@ -45,19 +46,20 @@ def tile_picked_haarinp_none_po_kernel(tc, x_words, x_scales, w1, w2_words, w2_s
         lb_sb = keep.tile([P, V // 16], U16, name="lb_sb")
         x_word_table = keep.tile([P, T], U32, name="x_word_table", align_bytes=64)
         x_scale_table = keep.tile([P, T], U8, name="x_scale_table", align_bytes=64)
-        w1_raw = tiles("w1_raw", 2, [P, PACK, H // 2], F32)
-        w2_word_raw = keep.tile([P, N], U32, name="w2_word_raw", align_bytes=64)
-        w2_scale_raw = keep.tile([P, N], U8, name="w2_scale_raw", align_bytes=64)
+        w1_raw = tiles("w1_raw", 2, [P, 2, H], F32)
+        w2_word_raw = shared.tile([P, N], U32, name="w2_word_raw", align_bytes=64, offset=0)
+        w2_scale_room = shared.tile([P, 4 * 4 * V], U8, name="w2_scale_room", align_bytes=64, offset=4 * N)
+        w2_scale_raw = w2_scale_room[:, :N]
 
         nc.vector.memset(x_scale_table[:].bitcast(I32), 0)
-        nc.vector.memset(w2_scale_raw[:].bitcast(I32), 0)
+        nc.vector.memset(w2_scale_raw.bitcast(I32), 0)
 
         w1_rows = w1.rearrange("(p j) c -> p j c", j=PACK)
         nc.sync.dma_start(offs_sb[:], offs)
         nc.sync.dma_start(out=x_word_table[:].bitcast(I32), in_=x_words[0].rearrange("p n t -> p (n t)").bitcast(I32))
         load_scale_rows(nc.sync, x_scale_table, x_scales[0])
         for h in range(2):
-            nc.sync.dma_start(out=w1_raw[h][:], in_=w1_rows[:, :, h * (H // 2) : (h + 1) * (H // 2)])
+            nc.sync.dma_start(out=w1_raw[h][:], in_=w1_rows[:, 2 * h : 2 * h + 2, :])
         nc.sync.dma_start(lb_sb[:], lb)
         nc.sync.dma_start(la_sb[:], la)
         nc.sync.dma_start(out=w2_word_raw[:].bitcast(I32), in_=w2_words[0].rearrange("p n t -> p (n t)").bitcast(I32))
@@ -73,15 +75,36 @@ def tile_picked_haarinp_none_po_kernel(tc, x_words, x_scales, w1, w2_words, w2_s
         w1_scale = tiles("w1_scale", PACK, [P, P], U8)
         for h in range(2):
             src = w1_raw[h][:].rearrange("p j (m e u) -> p u m j e", e=2, u=2)
-            ms = slice(h * (P // 2), (h + 1) * (P // 2))
-            nc.vector.tensor_copy(out=w1_grouped[0][:, :, ms, :].rearrange("p e m j -> p m j e"), in_=src[:, 0])
-            nc.scalar.copy(out=w1_grouped[1][:, :, ms, :].rearrange("p e m j -> p m j e"), in_=src[:, 1])
+            js = slice(2 * h, 2 * h + 2)
+            if h == 0:
+                nc.scalar.copy(out=w1_grouped[0][:, :, :, js].rearrange("p e m j -> p m j e"), in_=src[:, 0])
+            else:
+                for e in range(2):
+                    nc.vector.tensor_copy(out=w1_grouped[0][:, e, :, js], in_=src[:, 0, :, :, e])
+            nc.scalar.copy(out=w1_grouped[1][:, :, :, js].rearrange("p e m j -> p m j e"), in_=src[:, 1])
 
         y = tiles("y", PACK, [P, S], F32)
         z = [keep.tile([P, S], F32, name="z%d" % t, tag="z%d" % t, align_bytes=64) for t in range(PACK)]
         z_grouped = tiles("z_grouped", CHUNKS, [P, CHUNK, PACK], BF16)
         w2_codes = keep.tile([P, N], U32, name="w2_codes", align_bytes=64)
-        w2_scale = keep.tile([P, N], U8, name="w2_scale", align_bytes=64)
+        w2_scale = shared.tile([P, N], U8, name="w2_scale", align_bytes=64, offset=0)
+
+        kept = []
+
+        def warm_up(after):
+            mark = keep.tile([P, 1], F32, name="mark")
+            nc.scalar.activation(out=mark[:], in_=kept[0][:, 0:1], func=COPY, scale=after[:, 0:1])
+            warm = psum.tile([P, S], F32, name="warm", tag="late", bufs=1)
+            for i in range(2):
+                nc.tensor.matmul_mx(
+                    out=warm[:],
+                    lhsT=w1_codes[0][:].bitcast(FP8X4),
+                    lhsT_scale=w1_scale[0][:],
+                    rhs=x_word_picked[:].bitcast(FP8X4),
+                    rhs_scale=x_scale_picked[:],
+                    start=True,
+                    stop=True,
+                )
 
         def project(t):
             nc.vector.quantize_mx(
@@ -92,7 +115,11 @@ def tile_picked_haarinp_none_po_kernel(tc, x_words, x_scales, w1, w2_words, w2_s
             width = HALF if t == PLANE_ORDER[0] else S
             for first in range(0, S, width):
                 cols = slice(first, first + width)
-                acc = psum.tile([P, width], F32, name="acc", tag="bank")
+                if t == PLANE_ORDER[-1]:
+                    acc = psum.tile([P, width], F32, name="last_acc", tag="late", bufs=1)
+                    kept.append(acc)
+                else:
+                    acc = psum.tile([P, width], F32, name="acc", tag="bank")
                 nc.tensor.matmul_mx(
                     out=acc[:],
                     lhsT=w1_codes[t][:].bitcast(FP8X4),
@@ -111,18 +138,18 @@ def tile_picked_haarinp_none_po_kernel(tc, x_words, x_scales, w1, w2_words, w2_s
             )
             nc.vector.tensor_copy(
                 out=w2_scale[:].rearrange("p (t g i) -> p g t i", t=PACK, i=16),
-                in_=w2_scale_raw[:].rearrange("p (g i t) -> p g t i", t=PACK, i=16),
+                in_=w2_scale_raw.rearrange("p (g i t) -> p g t i", t=PACK, i=16),
             )
 
         def haar(pair):
             a, b, minus_b = {}, {}, {}
             for slot, t in enumerate(pair):
-                b[t] = keep.tile([P, V], F32, name="b%d" % t, tag="b%d" % slot, align_bytes=64)
+                b[t] = shared.tile([P, V], F32, name="b%d" % t, align_bytes=64, offset=4 * N + 8 * V * slot)
                 nc.vector.tensor_copy(out=b[t][:], in_=y[t][:].indirect(lb_sb[:]))
                 tag = "z%d" % PLANE_ORDER[0] if t == PLANE_ORDER[-1] else "minus_b%d" % t
                 minus_b[t] = keep.tile([P, V], F32, name="minus_b%d" % t, tag=tag, align_bytes=64)
                 nc.scalar.activation(out=minus_b[t][:], in_=b[t][:], func=COPY, scale=-1.0)
-                a[t] = keep.tile([P, V], F32, name="a%d" % t, tag="a%d" % slot, align_bytes=64)
+                a[t] = shared.tile([P, V], F32, name="a%d" % t, align_bytes=64, offset=4 * N + 8 * V * slot + 4 * V)
                 nc.vector.tensor_copy(out=a[t][:], in_=y[t][:].indirect(la_sb[:]))
             for t in pair:
                 nc.vector.tensor_tensor(z[t][:].indirect(la_sb[:]), a[t][:], b[t][:], ADD)
@@ -135,13 +162,15 @@ def tile_picked_haarinp_none_po_kernel(tc, x_words, x_scales, w1, w2_words, w2_s
                         nc.vector.tensor_copy(out=dst, in_=src)
                     else:
                         nc.scalar.copy(out=dst, in_=src)
+                    if t == PLANE_ORDER[-2] and c == 0:
+                        warm_up(z[t])
 
         for t in PLANE_ORDER[:2]:
             project(t)
-        haar(PLANE_ORDER[:2])
+        deal_w2()
         for t in PLANE_ORDER[2:]:
             project(t)
-        deal_w2()
+        haar(PLANE_ORDER[:2])
         haar(PLANE_ORDER[2:])
 
         z_codes = tiles("z_codes", CHUNKS, [P, CHUNK], U32)
@@ -161,19 +190,24 @@ def tile_picked_haarinp_none_po_kernel(tc, x_words, x_scales, w1, w2_words, w2_s
             )
         for c in range(CHUNKS):
             cols = slice(c * CHUNK, (c + 1) * CHUNK)
-            acc = psum.tile([P, PACK, CHUNK], F32, name="acc", tag="bank")
-            for t in range(PACK):
-                nc.tensor.matmul_mx(
-                    out=acc[:, t, :],
-                    lhsT=w2_codes[:, t * P : (t + 1) * P].bitcast(FP8X4),
-                    lhsT_scale=w2_scale[:, t * P : (t + 1) * P],
-                    rhs=z_codes[c][:].bitcast(FP8X4),
-                    rhs_scale=z_scale[c][:],
-                    start=True,
-                    stop=True,
-                )
-            nc.scalar.copy(out=result[c][:], in_=acc[:])
-            nc.sync.dma_start(out=out_rows[:, :, cols], in_=result[c][:])
+            group = 2 if c == 0 else PACK
+            for first in range(0, PACK, group):
+                acc = psum.tile([P, group, CHUNK], F32, name="acc", tag="bank")
+                for t in range(first, first + group):
+                    nc.tensor.matmul_mx(
+                        out=acc[:, t - first, :],
+                        lhsT=w2_codes[:, t * P : (t + 1) * P].bitcast(FP8X4),
+                        lhsT_scale=w2_scale[:, t * P : (t + 1) * P],
+                        rhs=z_codes[c][:].bitcast(FP8X4),
+                        rhs_scale=z_scale[c][:],
+                        start=True,
+                        stop=True,
+                    )
+                if c == 1:
+                    nc.vector.tensor_copy(out=result[c][:], in_=acc[:])
+                else:
+                    nc.scalar.copy(out=result[c][:, first : first + group, :], in_=acc[:])
+                nc.sync.dma_start(out=out_rows[:, first : first + group, cols], in_=result[c][:, first : first + group, :])
             if c == CHUNKS - 1:
                 nc.scalar.copy(out=result_grouped[c][:], in_=acc[:].rearrange("p t n -> p n t"))
             else:

@@ -45,49 +45,62 @@ def tile_picked_haarinp_none_po_kernel(tc, x_words, x_scales, w1, w2_words, w2_s
         la_sb = keep.tile([P, V // 16], U16, name="la_sb")
         lb_sb = keep.tile([P, V // 16], U16, name="lb_sb")
         x_word_table = keep.tile([P, T], U32, name="x_word_table", align_bytes=64)
-        x_scale_table = keep.tile([P, T], U8, name="x_scale_table", align_bytes=64)
+        x_scale_table = shared.tile([P, T], U8, name="x_scale_table", align_bytes=64, offset=0)
         w1_raw = tiles("w1_raw", 2, [P, 2, H], F32)
-        w2_word_raw = shared.tile([P, N], U32, name="w2_word_raw", align_bytes=64, offset=0)
-        w2_scale_room = shared.tile([P, 4 * 4 * V], U8, name="w2_scale_room", align_bytes=64, offset=4 * N)
-        w2_scale_raw = w2_scale_room[:, :N]
+        w2_scale_raw = keep.tile([P, N], U8, name="w2_scale_raw", align_bytes=64)
+        x_word_picked = keep.tile([P, S], U32, name="x_word_picked", align_bytes=64)
+        x_scale_gathered = keep.tile([P, S], U8, name="x_scale_gathered", align_bytes=64)
+        x_scale_picked = keep.tile([P, S], U8, name="x_scale_picked", align_bytes=64)
 
-        nc.vector.memset(x_scale_table[:].bitcast(I32), 0)
-        nc.vector.memset(w2_scale_raw.bitcast(I32), 0)
+        nc.vector.memset(w2_scale_raw[:].bitcast(I32), 0)
+        for first, stop in ((0, 16), (32, 64), (64, P)):
+            nc.vector.memset(x_scale_table[first:stop, :].bitcast(I32), 0)
+        nc.vector.memset(x_scale_picked[:].bitcast(I32), 0)
 
         w1_rows = w1.rearrange("(p j) c -> p j c", j=PACK)
+        nc.sync.dma_start(out=x_scale_table[16:32, :].bitcast(I32), in_=x_scales[0].bitcast(I32))
         nc.sync.dma_start(offs_sb[:], offs)
         nc.sync.dma_start(out=x_word_table[:].bitcast(I32), in_=x_words[0].rearrange("p n t -> p (n t)").bitcast(I32))
-        load_scale_rows(nc.sync, x_scale_table, x_scales[0])
+        load_scale_rows(nc.sync, w2_scale_raw, w2_scales[0])
         for h in range(2):
             nc.sync.dma_start(out=w1_raw[h][:], in_=w1_rows[:, 2 * h : 2 * h + 2, :])
         nc.sync.dma_start(lb_sb[:], lb)
         nc.sync.dma_start(la_sb[:], la)
-        nc.sync.dma_start(out=w2_word_raw[:].bitcast(I32), in_=w2_words[0].rearrange("p n t -> p (n t)").bitcast(I32))
-        load_scale_rows(nc.sync, w2_scale_raw, w2_scales[0])
 
-        x_word_picked = keep.tile([P, S], U32, name="x_word_picked", align_bytes=64)
-        x_scale_picked = keep.tile([P, S], U8, name="x_scale_picked", align_bytes=64)
+        nc.vector.tensor_copy(out=x_scale_gathered[:], in_=x_scale_table[:].indirect(offs_sb[:]))
+        for q in range(QUADS):
+            nc.sync.dma_start(
+                out=x_scale_picked[32 * q : 32 * q + 4, :].bitcast(I32),
+                in_=x_scale_gathered[16 + 4 * q : 20 + 4 * q, :].bitcast(I32),
+            )
+        w2_word_room = shared.tile([P, 4 * V], U32, name="w2_word_room", align_bytes=64, offset=0)
+        w2_word_raw = w2_word_room[:, :N]
+        nc.sync.dma_start(out=w2_word_raw.bitcast(I32), in_=w2_words[0].rearrange("p n t -> p (n t)").bitcast(I32))
         nc.vector.tensor_copy(out=x_word_picked[:], in_=x_word_table[:].indirect(offs_sb[:]))
-        nc.vector.tensor_copy(out=x_scale_picked[:], in_=x_scale_table[:].indirect(offs_sb[:]))
 
         w1_grouped = tiles("w1_grouped", 2, [P, 2, P, PACK], BF16)
         w1_codes = tiles("w1_codes", PACK, [P, P], U32)
         w1_scale = tiles("w1_scale", PACK, [P, P], U8)
+        w2_scale = keep.tile([P, N], U8, name="w2_scale", align_bytes=64)
         for h in range(2):
             src = w1_raw[h][:].rearrange("p j (m e u) -> p u m j e", e=2, u=2)
             js = slice(2 * h, 2 * h + 2)
             if h == 0:
-                nc.scalar.copy(out=w1_grouped[0][:, :, :, js].rearrange("p e m j -> p m j e"), in_=src[:, 0])
+                nc.vector.tensor_copy(out=w1_grouped[0][:, :, :, js].rearrange("p e m j -> p m j e"), in_=src[:, 0])
             else:
                 for e in range(2):
                     nc.vector.tensor_copy(out=w1_grouped[0][:, e, :, js], in_=src[:, 0, :, :, e])
             nc.scalar.copy(out=w1_grouped[1][:, :, :, js].rearrange("p e m j -> p m j e"), in_=src[:, 1])
+            if h == 0:
+                nc.vector.tensor_copy(
+                    out=w2_scale[:].rearrange("p (t g i) -> p g t i", t=PACK, i=16),
+                    in_=w2_scale_raw[:].rearrange("p (g i t) -> p g t i", t=PACK, i=16),
+                )
 
         y = tiles("y", PACK, [P, S], F32)
         z = [keep.tile([P, S], F32, name="z%d" % t, tag="z%d" % t, align_bytes=64) for t in range(PACK)]
         z_grouped = tiles("z_grouped", CHUNKS, [P, CHUNK, PACK], BF16)
         w2_codes = keep.tile([P, N], U32, name="w2_codes", align_bytes=64)
-        w2_scale = shared.tile([P, N], U8, name="w2_scale", align_bytes=64, offset=0)
 
         kept = []
 
@@ -134,22 +147,18 @@ def tile_picked_haarinp_none_po_kernel(tc, x_words, x_scales, w1, w2_words, w2_s
         def deal_w2():
             nc.vector.tensor_copy(
                 out=w2_codes[:].bitcast(I32).rearrange("p (t g i) -> p g t i", t=PACK, i=4),
-                in_=w2_word_raw[:].bitcast(I32).rearrange("p (g i t) -> p g t i", t=PACK, i=4),
-            )
-            nc.vector.tensor_copy(
-                out=w2_scale[:].rearrange("p (t g i) -> p g t i", t=PACK, i=16),
-                in_=w2_scale_raw.rearrange("p (g i t) -> p g t i", t=PACK, i=16),
+                in_=w2_word_raw.bitcast(I32).rearrange("p (g i t) -> p g t i", t=PACK, i=4),
             )
 
         def haar(pair):
             a, b, minus_b = {}, {}, {}
             for slot, t in enumerate(pair):
-                b[t] = shared.tile([P, V], F32, name="b%d" % t, align_bytes=64, offset=4 * N + 8 * V * slot)
+                b[t] = shared.tile([P, V], F32, name="b%d" % t, align_bytes=64, offset=8 * V * slot)
                 nc.vector.tensor_copy(out=b[t][:], in_=y[t][:].indirect(lb_sb[:]))
                 tag = "z%d" % PLANE_ORDER[0] if t == PLANE_ORDER[-1] else "minus_b%d" % t
                 minus_b[t] = keep.tile([P, V], F32, name="minus_b%d" % t, tag=tag, align_bytes=64)
                 nc.scalar.activation(out=minus_b[t][:], in_=b[t][:], func=COPY, scale=-1.0)
-                a[t] = shared.tile([P, V], F32, name="a%d" % t, align_bytes=64, offset=4 * N + 8 * V * slot + 4 * V)
+                a[t] = shared.tile([P, V], F32, name="a%d" % t, align_bytes=64, offset=8 * V * slot + 4 * V)
                 nc.vector.tensor_copy(out=a[t][:], in_=y[t][:].indirect(la_sb[:]))
             for t in pair:
                 nc.vector.tensor_tensor(z[t][:].indirect(la_sb[:]), a[t][:], b[t][:], ADD)
@@ -167,9 +176,9 @@ def tile_picked_haarinp_none_po_kernel(tc, x_words, x_scales, w1, w2_words, w2_s
 
         for t in PLANE_ORDER[:2]:
             project(t)
-        deal_w2()
         for t in PLANE_ORDER[2:]:
             project(t)
+        deal_w2()
         haar(PLANE_ORDER[:2])
         haar(PLANE_ORDER[2:])
 

@@ -36,7 +36,7 @@ def tile_picked_haarinp_none_po_kernel(tc, x_words, x_scales, w1, w2_words, w2_s
     with ExitStack() as ctx:
         keep = ctx.enter_context(tc.tile_pool(name="keep", bufs=1))
         shared = ctx.enter_context(tc.tile_pool(name="shared", bufs=1))
-        psum = ctx.enter_context(tc.psum_pool(name="psum", bufs=7))
+        psum = ctx.enter_context(tc.psum_pool(name="psum", bufs=8))
 
         def tiles(name, count, shape, dtype):
             return [keep.tile(shape, dtype, name="%s%d" % (name, i), align_bytes=64) for i in range(count)]
@@ -102,23 +102,6 @@ def tile_picked_haarinp_none_po_kernel(tc, x_words, x_scales, w1, w2_words, w2_s
         z_grouped = tiles("z_grouped", CHUNKS, [P, CHUNK, PACK], BF16)
         w2_codes = keep.tile([P, N], U32, name="w2_codes", align_bytes=64)
 
-        kept = []
-
-        def warm_up(after):
-            mark = keep.tile([P, 1], F32, name="mark")
-            nc.scalar.activation(out=mark[:], in_=kept[0][:, 0:1], func=COPY, scale=after[:, 0:1])
-            warm = psum.tile([P, S], F32, name="warm", tag="late", bufs=1)
-            for i in range(2):
-                nc.tensor.matmul_mx(
-                    out=warm[:],
-                    lhsT=w1_codes[0][:].bitcast(FP8X4),
-                    lhsT_scale=w1_scale[0][:],
-                    rhs=x_word_picked[:].bitcast(FP8X4),
-                    rhs_scale=x_scale_picked[:],
-                    start=True,
-                    stop=True,
-                )
-
         def project(t):
             nc.vector.quantize_mx(
                 out=w1_codes[t][:].bitcast(FP8X4),
@@ -128,11 +111,7 @@ def tile_picked_haarinp_none_po_kernel(tc, x_words, x_scales, w1, w2_words, w2_s
             width = HALF if t == PLANE_ORDER[0] else S
             for first in range(0, S, width):
                 cols = slice(first, first + width)
-                if t == PLANE_ORDER[-1]:
-                    acc = psum.tile([P, width], F32, name="last_acc", tag="late", bufs=1)
-                    kept.append(acc)
-                else:
-                    acc = psum.tile([P, width], F32, name="acc", tag="bank")
+                acc = psum.tile([P, width], F32, name="acc", tag="bank")
                 nc.tensor.matmul_mx(
                     out=acc[:],
                     lhsT=w1_codes[t][:].bitcast(FP8X4),
@@ -171,8 +150,6 @@ def tile_picked_haarinp_none_po_kernel(tc, x_words, x_scales, w1, w2_words, w2_s
                         nc.vector.tensor_copy(out=dst, in_=src)
                     else:
                         nc.scalar.copy(out=dst, in_=src)
-                    if t == PLANE_ORDER[-2] and c == 0:
-                        warm_up(z[t])
 
         for t in PLANE_ORDER[:2]:
             project(t)

@@ -13,6 +13,7 @@ U8 = mybir.dt.uint8
 FP8X4 = mybir.dt.float8_e4m3fn_x4
 COPY = mybir.ActivationFunctionType.Copy
 ADD = mybir.AluOpType.add
+SUB = mybir.AluOpType.subtract
 
 P = 128
 PACK = 4
@@ -97,7 +98,7 @@ def tile_picked_haarinp_none_po_kernel(tc, x_words, x_scales, w1, w2_words, w2_s
                     in_=w2_scale_raw[:].rearrange("p (g i t) -> p g t i", t=PACK, i=16),
                 )
 
-        y = tiles("y", PACK, [P, S], F32)
+        y = [keep.tile([P, S], F32, name="y%d" % t, tag="y%d" % t, align_bytes=64) for t in range(PACK)]
         z = [keep.tile([P, S], F32, name="z%d" % t, tag="z%d" % t, align_bytes=64) for t in range(PACK)]
         z_grouped = tiles("z_grouped", CHUNKS, [P, CHUNK, PACK], BF16)
         w2_codes = keep.tile([P, N], U32, name="w2_codes", align_bytes=64)
@@ -129,20 +130,28 @@ def tile_picked_haarinp_none_po_kernel(tc, x_words, x_scales, w1, w2_words, w2_s
                 in_=w2_word_raw.bitcast(I32).rearrange("p (g i t) -> p g t i", t=PACK, i=4),
             )
 
-        def haar(pair):
-            a, b, minus_b = {}, {}, {}
-            for slot, t in enumerate(pair):
-                b[t] = shared.tile([P, V], F32, name="b%d" % t, align_bytes=64, offset=8 * V * slot)
-                nc.vector.tensor_copy(out=b[t][:], in_=y[t][:].indirect(lb_sb[:]))
-                tag = "z%d" % PLANE_ORDER[0] if t == PLANE_ORDER[-1] else "minus_b%d" % t
-                minus_b[t] = keep.tile([P, V], F32, name="minus_b%d" % t, tag=tag, align_bytes=64)
-                nc.scalar.activation(out=minus_b[t][:], in_=b[t][:], func=COPY, scale=-1.0)
-                a[t] = shared.tile([P, V], F32, name="a%d" % t, align_bytes=64, offset=8 * V * slot + 4 * V)
-                nc.vector.tensor_copy(out=a[t][:], in_=y[t][:].indirect(la_sb[:]))
+        a, b, total, difference = {}, {}, {}, {}
+
+        def fetch(slot, t):
+            b[t] = shared.tile([P, V], F32, name="b%d" % t, align_bytes=64, offset=8 * V * slot)
+            nc.vector.tensor_copy(out=b[t][:], in_=y[t][:].indirect(lb_sb[:]))
+            a[t] = shared.tile([P, V], F32, name="a%d" % t, align_bytes=64, offset=8 * V * slot + 4 * V)
+            nc.vector.tensor_copy(out=a[t][:], in_=y[t][:].indirect(la_sb[:]))
+
+        def combine(pair):
             for t in pair:
-                nc.vector.tensor_tensor(z[t][:].indirect(la_sb[:]), a[t][:], b[t][:], ADD)
+                total[t] = keep.tile([P, V], F32, name="total%d" % t, align_bytes=64)
+                nc.gpsimd.tensor_tensor(total[t][:], a[t][:], b[t][:], ADD)
             for t in pair:
-                nc.vector.tensor_tensor(z[t][:].indirect(lb_sb[:]), a[t][:], minus_b[t][:], ADD)
+                tag = "z%d" % PLANE_ORDER[0] if t == PLANE_ORDER[-1] else "y%d" % pair[1] if t == pair[0] else "difference%d" % t
+                difference[t] = keep.tile([P, V], F32, name="difference%d" % t, tag=tag, align_bytes=64)
+                nc.gpsimd.tensor_tensor(difference[t][:], a[t][:], b[t][:], SUB)
+
+        def put_back(pair):
+            for t in pair:
+                nc.vector.tensor_copy(out=z[t][:].indirect(la_sb[:]), in_=total[t][:])
+            for t in pair:
+                nc.vector.tensor_copy(out=z[t][:].indirect(lb_sb[:]), in_=difference[t][:])
                 for c in range(CHUNKS):
                     dst = z_grouped[c][:, :, t]
                     src = z[t][:, c * CHUNK : (c + 1) * CHUNK]
@@ -156,8 +165,11 @@ def tile_picked_haarinp_none_po_kernel(tc, x_words, x_scales, w1, w2_words, w2_s
         for t in PLANE_ORDER[2:]:
             project(t)
         deal_w2()
-        haar(PLANE_ORDER[:2])
-        haar(PLANE_ORDER[2:])
+        for slot, t in enumerate(PLANE_ORDER):
+            fetch(slot, t)
+        for pair in (PLANE_ORDER[:2], PLANE_ORDER[2:]):
+            combine(pair)
+            put_back(pair)
 
         z_codes = tiles("z_codes", CHUNKS, [P, CHUNK], U32)
         z_scale = tiles("z_scale", CHUNKS, [P, CHUNK], U8)

@@ -82,7 +82,7 @@ def tile_picked_haarinp_none_po_kernel(tc, x_words, x_scales, w1, w2_words, w2_s
         w1_grouped = tiles("w1_grouped", 2, [P, 2, P, PACK], BF16)
         w1_codes = tiles("w1_codes", PACK, [P, P], U32)
         w1_scale = tiles("w1_scale", PACK, [P, P], U8)
-        w2_scale = keep.tile([P, N], U8, name="w2_scale", align_bytes=64)
+        w2_scale_early = keep.tile([P, N - P], U8, name="w2_scale_early", align_bytes=64)
         for h in range(2):
             src = w1_raw[h][:].rearrange("p j (m e u) -> p u m j e", e=2, u=2)
             js = slice(2 * h, 2 * h + 2)
@@ -94,8 +94,8 @@ def tile_picked_haarinp_none_po_kernel(tc, x_words, x_scales, w1, w2_words, w2_s
             nc.scalar.copy(out=w1_grouped[1][:, :, :, js].rearrange("p e m j -> p m j e"), in_=src[:, 1])
             if h == 0:
                 nc.vector.tensor_copy(
-                    out=w2_scale[:].rearrange("p (t g i) -> p g t i", t=PACK, i=16),
-                    in_=w2_scale_raw[:].rearrange("p (g i t) -> p g t i", t=PACK, i=16),
+                    out=w2_scale_early[:].rearrange("p (t g i) -> p g t i", t=PACK - 1, i=16),
+                    in_=w2_scale_raw[:].rearrange("p (g i t) -> p g t i", t=PACK, i=16)[:, :, : PACK - 1, :],
                 )
 
         y = [keep.tile([P, S], F32, name="y%d" % t, tag="y%d" % t, align_bytes=64) for t in range(PACK)]
@@ -171,6 +171,10 @@ def tile_picked_haarinp_none_po_kernel(tc, x_words, x_scales, w1, w2_words, w2_s
             combine(pair)
             put_back(pair)
 
+        w2_scale_last = keep.tile([P, P], U8, name="w2_scale_last", tag="y%d" % PLANE_ORDER[-1], align_bytes=64)
+        nc.gpsimd.tensor_copy(out=w2_scale_last[:], in_=w2_scale_raw[:].rearrange("p (m t) -> p m t", t=PACK)[:, :, PACK - 1])
+        w2_scale = [w2_scale_early[:, t * P : (t + 1) * P] for t in range(PACK - 1)] + [w2_scale_last[:]]
+
         z_codes = tiles("z_codes", CHUNKS, [P, CHUNK], U32)
         z_scale = tiles("z_scale", CHUNKS, [P, CHUNK], U8)
         result = tiles("result", CHUNKS, [P, PACK, CHUNK], F32)
@@ -195,7 +199,7 @@ def tile_picked_haarinp_none_po_kernel(tc, x_words, x_scales, w1, w2_words, w2_s
                     nc.tensor.matmul_mx(
                         out=acc[:, t - first, :],
                         lhsT=w2_codes[:, t * P : (t + 1) * P].bitcast(FP8X4),
-                        lhsT_scale=w2_scale[:, t * P : (t + 1) * P],
+                        lhsT_scale=w2_scale[t],
                         rhs=z_codes[c][:].bitcast(FP8X4),
                         rhs_scale=z_scale[c][:],
                         start=True,

@@ -175,6 +175,18 @@ def tile_picked_haarinp_none_po_kernel(tc, x_words, x_scales, w1, w2_words, w2_s
         nc.gpsimd.tensor_copy(out=w2_scale_last[:], in_=w2_scale_raw[:].rearrange("p (m t) -> p m t", t=PACK)[:, :, PACK - 1])
         w2_scale = [w2_scale_early[:, t * P : (t + 1) * P] for t in range(PACK - 1)] + [w2_scale_last[:]]
 
+        warm = psum.tile([P, S], F32, name="warm", tag="bank")
+        for repeat in range(2):
+            nc.tensor.matmul_mx(
+                out=warm[:],
+                lhsT=w2_codes[:, N - P :].bitcast(FP8X4),
+                lhsT_scale=w2_scale_last[:],
+                rhs=x_word_picked[:].bitcast(FP8X4),
+                rhs_scale=x_scale_picked[:],
+                start=True,
+                stop=True,
+            )
+
         z_codes = tiles("z_codes", CHUNKS, [P, CHUNK], U32)
         z_scale = tiles("z_scale", CHUNKS, [P, CHUNK], U8)
         result = tiles("result", CHUNKS, [P, PACK, CHUNK], F32)

@@ -14,6 +14,7 @@ FP8X4 = mybir.dt.float8_e4m3fn_x4
 COPY = mybir.ActivationFunctionType.Copy
 ADD = mybir.AluOpType.add
 SUB = mybir.AluOpType.subtract
+MULT = mybir.AluOpType.mult
 
 P = 128
 PACK = 4
@@ -37,6 +38,7 @@ def tile_picked_haarinp_none_po_kernel(tc, x_words, x_scales, w1, w2_words, w2_s
     with ExitStack() as ctx:
         keep = ctx.enter_context(tc.tile_pool(name="keep", bufs=1))
         shared = ctx.enter_context(tc.tile_pool(name="shared", bufs=1))
+        ring = ctx.enter_context(tc.tile_pool(name="ring", bufs=1))
         psum = ctx.enter_context(tc.psum_pool(name="psum", bufs=8))
 
         def tiles(name, count, shape, dtype):
@@ -74,15 +76,14 @@ def tile_picked_haarinp_none_po_kernel(tc, x_words, x_scales, w1, w2_words, w2_s
                 out=x_scale_picked[32 * q : 32 * q + 4, :].bitcast(I32),
                 in_=x_scale_gathered[16 + 4 * q : 20 + 4 * q, :].bitcast(I32),
             )
-        w2_word_room = shared.tile([P, 4 * V], U32, name="w2_word_room", align_bytes=64, offset=0)
-        w2_word_raw = w2_word_room[:, :N]
-        nc.sync.dma_start(out=w2_word_raw.bitcast(I32), in_=w2_words[0].rearrange("p n t -> p (n t)").bitcast(I32))
+        w2_word_raw = shared.tile([P, N], U32, name="w2_word_raw", align_bytes=64, offset=0)
+        nc.sync.dma_start(out=w2_word_raw[:].bitcast(I32), in_=w2_words[0].rearrange("p n t -> p (n t)").bitcast(I32))
         nc.vector.tensor_copy(out=x_word_picked[:], in_=x_word_table[:].indirect(offs_sb[:]))
 
         w1_grouped = tiles("w1_grouped", 2, [P, 2, P, PACK], BF16)
         w1_codes = tiles("w1_codes", PACK, [P, P], U32)
         w1_scale = tiles("w1_scale", PACK, [P, P], U8)
-        w2_scale_early = keep.tile([P, N - P], U8, name="w2_scale_early", align_bytes=64)
+        w2_scale_dealt = keep.tile([P, N], U8, name="w2_scale_dealt", align_bytes=64)
         for h in range(2):
             src = w1_raw[h][:].rearrange("p j (m e u) -> p u m j e", e=2, u=2)
             js = slice(2 * h, 2 * h + 2)
@@ -94,22 +95,21 @@ def tile_picked_haarinp_none_po_kernel(tc, x_words, x_scales, w1, w2_words, w2_s
             nc.scalar.copy(out=w1_grouped[1][:, :, :, js].rearrange("p e m j -> p m j e"), in_=src[:, 1])
             if h == 0:
                 nc.vector.tensor_copy(
-                    out=w2_scale_early[:].rearrange("p (t g i) -> p g t i", t=PACK - 1, i=16),
-                    in_=w2_scale_raw[:].rearrange("p (g i t) -> p g t i", t=PACK, i=16)[:, :, : PACK - 1, :],
+                    out=w2_scale_dealt[:].rearrange("p (t g i) -> p g t i", t=PACK, i=16),
+                    in_=w2_scale_raw[:].rearrange("p (g i t) -> p g t i", t=PACK, i=16),
                 )
 
-        y = [keep.tile([P, S], F32, name="y%d" % t, tag="y%d" % t, align_bytes=64) for t in range(PACK)]
         z = [keep.tile([P, S], F32, name="z%d" % t, tag="z%d" % t, align_bytes=64) for t in range(PACK)]
-        z_grouped = tiles("z_grouped", CHUNKS, [P, CHUNK, PACK], BF16)
-        w2_codes = keep.tile([P, N], U32, name="w2_codes", align_bytes=64)
 
-        def project(t):
+        banks = {}
+
+        def project(slot, t):
             nc.vector.quantize_mx(
                 out=w1_codes[t][:].bitcast(FP8X4),
                 scales=w1_scale[t][:],
                 in_=w1_grouped[t % 2][:, t // 2].rearrange("p m j -> p (m j)"),
             )
-            width = HALF if t == PLANE_ORDER[0] else S
+            width = (CHUNK, HALF, S, S)[slot]
             for first in range(0, S, width):
                 cols = slice(first, first + width)
                 acc = psum.tile([P, width], F32, name="acc", tag="bank")
@@ -122,70 +122,84 @@ def tile_picked_haarinp_none_po_kernel(tc, x_words, x_scales, w1, w2_words, w2_s
                     start=True,
                     stop=True,
                 )
+                banks.setdefault(t, []).append((cols, acc))
+
+        y, a, b, minus_b = {}, {}, {}, {}
+        y_offset = (9280, 2048, 4032, 6016)
+        minus_b_offset = {0: 1088, 2: 6208}
+        z_grouped_offset = (4160, 7232)
+
+        def fetch(slot):
+            t = PLANE_ORDER[slot]
+            y[t] = ring.tile([P, S], F32, name="y%d" % t, align_bytes=64, offset=y_offset[slot])
+            for cols, acc in banks[t]:
                 nc.scalar.activation(out=y[t][:, cols], in_=acc[:], func=COPY, scale=0.75)
+            a[t] = keep.tile([P, V], F32, name="a%d" % t, align_bytes=64)
+            nc.scalar.activation(out=a[t][:], in_=y[t][:].indirect(la_sb[:]), func=COPY)
+            b[t] = keep.tile([P, V], F32, name="b%d" % t, align_bytes=64)
+            if slot == 0:
+                nc.vector.tensor_copy(out=b[t][:], in_=y[t][:].indirect(lb_sb[:]))
+            else:
+                nc.scalar.activation(out=b[t][:], in_=y[t][:].indirect(lb_sb[:]), func=COPY)
 
-        def deal_w2():
-            nc.vector.tensor_copy(
-                out=w2_codes[:].bitcast(I32).rearrange("p (t g i) -> p g t i", t=PACK, i=4),
-                in_=w2_word_raw.bitcast(I32).rearrange("p (g i t) -> p g t i", t=PACK, i=4),
-            )
+        def put_sum(slot):
+            t = PLANE_ORDER[slot]
+            nc.vector.tensor_tensor(z[t][:].indirect(la_sb[:]), a[t][:], b[t][:], ADD)
 
-        a, b, total, difference = {}, {}, {}, {}
+        def negate(slot):
+            t = PLANE_ORDER[slot]
+            if slot in minus_b_offset:
+                minus_b[t] = ring.tile([P, V], F32, name="minus_b%d" % t, align_bytes=64, offset=minus_b_offset[slot])
+            else:
+                tag = "z%d" % PLANE_ORDER[0] if slot == PACK - 1 else "minus_b%d" % t
+                minus_b[t] = keep.tile([P, V], F32, name="minus_b%d" % t, tag=tag, align_bytes=64)
+            nc.scalar.activation(out=minus_b[t][:], in_=b[t][:], func=COPY, scale=-1.0)
 
-        def fetch(slot, t):
-            b[t] = shared.tile([P, V], F32, name="b%d" % t, align_bytes=64, offset=8 * V * slot)
-            nc.vector.tensor_copy(out=b[t][:], in_=y[t][:].indirect(lb_sb[:]))
-            a[t] = shared.tile([P, V], F32, name="a%d" % t, align_bytes=64, offset=8 * V * slot + 4 * V)
-            nc.vector.tensor_copy(out=a[t][:], in_=y[t][:].indirect(la_sb[:]))
+        def put_difference(slot):
+            t = PLANE_ORDER[slot]
+            nc.vector.tensor_tensor(z[t][:].indirect(lb_sb[:]), a[t][:], minus_b[t][:], ADD)
 
-        def combine(pair):
-            for t in pair:
-                total[t] = keep.tile([P, V], F32, name="total%d" % t, align_bytes=64)
-                nc.gpsimd.tensor_tensor(total[t][:], a[t][:], b[t][:], ADD)
-            for t in pair:
-                tag = "z%d" % PLANE_ORDER[0] if t == PLANE_ORDER[-1] else "y%d" % pair[1] if t == pair[0] else "difference%d" % t
-                difference[t] = keep.tile([P, V], F32, name="difference%d" % t, tag=tag, align_bytes=64)
-                nc.gpsimd.tensor_tensor(difference[t][:], a[t][:], b[t][:], SUB)
+        def regroup(slot):
+            t = PLANE_ORDER[slot]
+            for h in range(2):
+                if slot < PACK - 1:
+                    nc.scalar.copy(out=z_grouped[h][:, :, t], in_=z[t][:, h * HALF : (h + 1) * HALF])
+                else:
+                    engine_copy = nc.vector.tensor_copy if h == 0 else nc.scalar.copy
+                    for first in range(0, HALF, CHUNK):
+                        engine_copy(
+                            out=z_grouped[h][:, first : first + CHUNK, t],
+                            in_=z[t][:, h * HALF + first : h * HALF + first + CHUNK],
+                        )
 
-        def put_back(pair):
-            for t in pair:
-                nc.vector.tensor_copy(out=z[t][:].indirect(la_sb[:]), in_=total[t][:])
-            for t in pair:
-                nc.vector.tensor_copy(out=z[t][:].indirect(lb_sb[:]), in_=difference[t][:])
-                for c in range(CHUNKS):
-                    dst = z_grouped[c][:, :, t]
-                    src = z[t][:, c * CHUNK : (c + 1) * CHUNK]
-                    if t == PLANE_ORDER[-1] and c < CHUNKS // 2:
-                        nc.vector.tensor_copy(out=dst, in_=src)
-                    else:
-                        nc.scalar.copy(out=dst, in_=src)
-
-        for t in PLANE_ORDER[:2]:
-            project(t)
-        for t in PLANE_ORDER[2:]:
-            project(t)
-        deal_w2()
         for slot, t in enumerate(PLANE_ORDER):
-            fetch(slot, t)
-        for pair in (PLANE_ORDER[:2], PLANE_ORDER[2:]):
-            combine(pair)
-            put_back(pair)
+            project(slot, t)
+        for slot in (0, 1):
+            fetch(slot)
+            put_sum(slot)
+        for slot in (0, 1):
+            negate(slot)
+            put_difference(slot)
+        for slot in (2, 3):
+            fetch(slot)
+            put_sum(slot)
+        negate(2)
+        put_difference(2)
+        w2_codes = ring.tile([P, N], U32, name="w2_codes", align_bytes=64, offset=2112)
+        dealt = w2_codes[:].rearrange("p (t g i) -> p g t i", t=PACK, i=LINE)
+        raw = w2_word_raw[:].rearrange("p (g i t) -> p g t i", t=PACK, i=LINE)
+        for first in range(0, P // LINE, 8):
+            nc.scalar.copy(out=dealt[:, first : first + 8], in_=raw[:, first : first + 8])
+        z_grouped = [
+            ring.tile([P, HALF, PACK], BF16, name="z_grouped%d" % h, align_bytes=64, offset=z_grouped_offset[h]) for h in range(2)
+        ]
+        regroup(0)
+        negate(PACK - 1)
+        put_difference(PACK - 1)
+        for slot in range(1, PACK):
+            regroup(slot)
 
-        w2_scale_last = keep.tile([P, P], U8, name="w2_scale_last", tag="y%d" % PLANE_ORDER[-1], align_bytes=64)
-        nc.gpsimd.tensor_copy(out=w2_scale_last[:], in_=w2_scale_raw[:].rearrange("p (m t) -> p m t", t=PACK)[:, :, PACK - 1])
-        w2_scale = [w2_scale_early[:, t * P : (t + 1) * P] for t in range(PACK - 1)] + [w2_scale_last[:]]
-
-        warm = psum.tile([P, S], F32, name="warm", tag="bank")
-        for repeat in range(2):
-            nc.tensor.matmul_mx(
-                out=warm[:],
-                lhsT=w2_codes[:, N - P :].bitcast(FP8X4),
-                lhsT_scale=w2_scale_last[:],
-                rhs=x_word_picked[:].bitcast(FP8X4),
-                rhs_scale=x_scale_picked[:],
-                start=True,
-                stop=True,
-            )
+        w2_scale = [w2_scale_dealt[:, t * P : (t + 1) * P] for t in range(PACK)]
 
         z_codes = tiles("z_codes", CHUNKS, [P, CHUNK], U32)
         z_scale = tiles("z_scale", CHUNKS, [P, CHUNK], U8)
@@ -200,14 +214,14 @@ def tile_picked_haarinp_none_po_kernel(tc, x_words, x_scales, w1, w2_words, w2_s
             nc.vector.quantize_mx(
                 out=z_codes[c][:].bitcast(FP8X4),
                 scales=z_scale[c][:],
-                in_=z_grouped[c][:].rearrange("p n t -> p (n t)"),
+                in_=z_grouped[c // 2][:, (c % 2) * CHUNK : (c % 2 + 1) * CHUNK, :].rearrange("p n t -> p (n t)"),
             )
         for c in range(CHUNKS):
             cols = slice(c * CHUNK, (c + 1) * CHUNK)
-            group = 2 if c == 0 else PACK
-            for first in range(0, PACK, group):
-                acc = psum.tile([P, group, CHUNK], F32, name="acc", tag="bank")
-                for t in range(first, first + group):
+            for first in range(0, PACK, 2):
+                planes = slice(first, first + 2)
+                acc = psum.tile([P, 2, CHUNK], F32, name="acc", tag="bank")
+                for t in range(first, first + 2):
                     nc.tensor.matmul_mx(
                         out=acc[:, t - first, :],
                         lhsT=w2_codes[:, t * P : (t + 1) * P].bitcast(FP8X4),
@@ -217,18 +231,12 @@ def tile_picked_haarinp_none_po_kernel(tc, x_words, x_scales, w1, w2_words, w2_s
                         start=True,
                         stop=True,
                     )
-                if c == 1:
-                    nc.vector.tensor_copy(out=result[c][:], in_=acc[:])
-                else:
-                    nc.scalar.copy(out=result[c][:, first : first + group, :], in_=acc[:])
-                nc.sync.dma_start(out=out_rows[:, first : first + group, cols], in_=result[c][:, first : first + group, :])
-            if c == CHUNKS - 1:
-                nc.scalar.copy(out=result_grouped[c][:], in_=acc[:].rearrange("p t n -> p n t"))
-            else:
-                nc.vector.tensor_copy(
-                    out=result_grouped[c][:].rearrange("p (g i) t -> p g t i", i=LINE),
-                    in_=result[c][:].rearrange("p t (g i) -> p g t i", i=LINE),
-                )
+                nc.scalar.copy(out=result[c][:, planes, :], in_=acc[:])
+            nc.sync.dma_start(out=out_rows[:, :, cols], in_=result[c][:])
+            nc.vector.tensor_copy(
+                out=result_grouped[c][:].rearrange("p (g i) t -> p g t i", i=LINE),
+                in_=result[c][:].rearrange("p t (g i) -> p g t i", i=LINE),
+            )
             nc.vector.quantize_mx(
                 out=out_codes[:, cols].bitcast(FP8X4),
                 scales=out_scale[:, cols],

@@ -13,242 +13,218 @@ U8 = mybir.dt.uint8
 FP8X4 = mybir.dt.float8_e4m3fn_x4
 COPY = mybir.ActivationFunctionType.Copy
 ADD = mybir.AluOpType.add
-SUB = mybir.AluOpType.subtract
-MULT = mybir.AluOpType.mult
 
 P = 128
 PACK = 4
 QUADS = 4
-HALF = S // 2
 CHUNK = 128
 CHUNKS = S // CHUNK
 LINE = 4
+LIST = 16
 PLANE_ORDER = (0, 2, 3, 1)
 
 FLOPS = 2 * K * H * S + 2 * H * N * S
 
 
-def load_scale_rows(queue, plane, rows):
+def quantize(nc, codes, scale, values):
+    nc.vector.quantize_mx(out=codes.bitcast(FP8X4), scales=scale, in_=values.rearrange("p n t -> p (n t)"))
+
+
+def product(nc, acc, w_codes, w_scale, codes, scale):
+    nc.tensor.matmul_mx(
+        out=acc, lhsT=w_codes.bitcast(FP8X4), lhsT_scale=w_scale, rhs=codes.bitcast(FP8X4), rhs_scale=scale, start=True, stop=True
+    )
+
+
+def move_scale_rows(nc, plane, rows, first):
     for q in range(QUADS):
-        queue.dma_start(out=plane[32 * q : 32 * q + 4, :].bitcast(I32), in_=rows[4 * q : 4 * q + 4, :].bitcast(I32))
+        nc.sync.dma_start(out=plane[32 * q : 32 * q + 4, :].bitcast(I32), in_=rows[first + 4 * q : first + 4 * q + 4, :].bitcast(I32))
 
 
 def tile_picked_haarinp_none_po_kernel(tc, x_words, x_scales, w1, w2_words, w2_scales, offs, la, lb, out_0, out_1, out_2):
     nc = tc.nc
     with ExitStack() as ctx:
         keep = ctx.enter_context(tc.tile_pool(name="keep", bufs=1))
-        shared = ctx.enter_context(tc.tile_pool(name="shared", bufs=1))
-        ring = ctx.enter_context(tc.tile_pool(name="ring", bufs=1))
-        psum = ctx.enter_context(tc.psum_pool(name="psum", bufs=8))
+        reuse = ctx.enter_context(tc.tile_pool(name="reuse", bufs=1))
+        psum = ctx.enter_context(tc.psum_pool(name="psum", bufs=1))
+
+        def tile(name, shape, dtype, tag=None):
+            return keep.tile(shape, dtype, name=name, tag=tag or name, align_bytes=64)
 
         def tiles(name, count, shape, dtype):
-            return [keep.tile(shape, dtype, name="%s%d" % (name, i), align_bytes=64) for i in range(count)]
+            return [tile("%s%d" % (name, i), shape, dtype) for i in range(count)]
 
-        offs_sb = keep.tile([P, S // 16], U16, name="offs_sb")
-        la_sb = keep.tile([P, V // 16], U16, name="la_sb")
-        lb_sb = keep.tile([P, V // 16], U16, name="lb_sb")
-        x_word_table = keep.tile([P, T], U32, name="x_word_table", align_bytes=64)
-        x_scale_table = shared.tile([P, T], U8, name="x_scale_table", align_bytes=64, offset=0)
-        w1_raw = tiles("w1_raw", 2, [P, 2, H], F32)
-        w2_scale_raw = keep.tile([P, N], U8, name="w2_scale_raw", align_bytes=64)
-        x_word_picked = keep.tile([P, S], U32, name="x_word_picked", align_bytes=64)
-        x_scale_gathered = keep.tile([P, S], U8, name="x_scale_gathered", align_bytes=64)
-        x_scale_picked = keep.tile([P, S], U8, name="x_scale_picked", align_bytes=64)
+        offs_sb = keep.tile([P, S // LIST], U16, name="offs_sb")
+        la_sb = keep.tile([P, V // LIST], U16, name="la_sb")
+        lb_sb = keep.tile([P, V // LIST], U16, name="lb_sb")
+        x_word_table = tile("x_word_table", [P, T], U32)
+        x_scale_table = tile("x_scale_table", [P, T], U8, tag="x_scale_table")
+        x_word_picked = tile("x_word_picked", [P, S], U32)
+        x_scale_gathered = tile("x_scale_gathered", [P, S], U8)
+        x_scale_picked = tile("x_scale_picked", [P, S], U8)
+        w1_early = tile("w1_early", [P, PACK - 1, H], F32)
+        w1_late = tile("w1_late", [P, H], F32)
+        w2_scale_raw = tile("w2_scale_raw", [P, N], U8)
+        w2_scale_dealt = tile("w2_scale_dealt", [P, N], U8)
+        w2_scale = tile("w2_scale", [P, N], U8)
 
-        nc.vector.memset(w2_scale_raw[:].bitcast(I32), 0)
         for first, stop in ((0, 16), (32, 64), (64, P)):
             nc.vector.memset(x_scale_table[first:stop, :].bitcast(I32), 0)
+        nc.vector.memset(w2_scale_raw[:].bitcast(I32), 0)
         nc.vector.memset(x_scale_picked[:].bitcast(I32), 0)
+        nc.vector.memset(w2_scale[:].bitcast(I32), 0)
 
         w1_rows = w1.rearrange("(p j) c -> p j c", j=PACK)
         nc.sync.dma_start(out=x_scale_table[16:32, :].bitcast(I32), in_=x_scales[0].bitcast(I32))
         nc.sync.dma_start(offs_sb[:], offs)
         nc.sync.dma_start(out=x_word_table[:].bitcast(I32), in_=x_words[0].rearrange("p n t -> p (n t)").bitcast(I32))
-        load_scale_rows(nc.sync, w2_scale_raw, w2_scales[0])
-        for h in range(2):
-            nc.sync.dma_start(out=w1_raw[h][:], in_=w1_rows[:, 2 * h : 2 * h + 2, :])
-        nc.sync.dma_start(lb_sb[:], lb)
+        nc.sync.dma_start(out=w2_scale_raw[0:16, :].bitcast(I32), in_=w2_scales[0].bitcast(I32))
+        nc.sync.dma_start(out=w1_early[:], in_=w1_rows[:, : PACK - 1, :])
+        nc.sync.dma_start(out=w1_late[:], in_=w1_rows[:, PACK - 1, :])
         nc.sync.dma_start(la_sb[:], la)
+        nc.sync.dma_start(lb_sb[:], lb)
 
         nc.vector.tensor_copy(out=x_scale_gathered[:], in_=x_scale_table[:].indirect(offs_sb[:]))
-        for q in range(QUADS):
-            nc.sync.dma_start(
-                out=x_scale_picked[32 * q : 32 * q + 4, :].bitcast(I32),
-                in_=x_scale_gathered[16 + 4 * q : 20 + 4 * q, :].bitcast(I32),
-            )
-        w2_word_raw = shared.tile([P, N], U32, name="w2_word_raw", align_bytes=64, offset=0)
+        move_scale_rows(nc, x_scale_picked, x_scale_gathered, 16)
+        w2_word_raw = tile("w2_word_raw", [P, N], U32, tag="x_scale_table")
         nc.sync.dma_start(out=w2_word_raw[:].bitcast(I32), in_=w2_words[0].rearrange("p n t -> p (n t)").bitcast(I32))
         nc.vector.tensor_copy(out=x_word_picked[:], in_=x_word_table[:].indirect(offs_sb[:]))
+        nc.vector.tensor_copy(
+            out=w2_scale_dealt[:].rearrange("p (t g i) -> p g t i", t=PACK, i=16),
+            in_=w2_scale_raw[:].rearrange("p (g i t) -> p g t i", t=PACK, i=16),
+        )
+        move_scale_rows(nc, w2_scale, w2_scale_dealt, 0)
 
         w1_grouped = tiles("w1_grouped", 2, [P, 2, P, PACK], BF16)
         w1_codes = tiles("w1_codes", PACK, [P, P], U32)
         w1_scale = tiles("w1_scale", PACK, [P, P], U8)
-        w2_scale_dealt = keep.tile([P, N], U8, name="w2_scale_dealt", align_bytes=64)
-        for h in range(2):
-            src = w1_raw[h][:].rearrange("p j (m e u) -> p u m j e", e=2, u=2)
-            js = slice(2 * h, 2 * h + 2)
-            if h == 0:
-                nc.vector.tensor_copy(out=w1_grouped[0][:, :, :, js].rearrange("p e m j -> p m j e"), in_=src[:, 0])
-            else:
-                for e in range(2):
-                    nc.vector.tensor_copy(out=w1_grouped[0][:, e, :, js], in_=src[:, 0, :, :, e])
-            nc.scalar.copy(out=w1_grouped[1][:, :, :, js].rearrange("p e m j -> p m j e"), in_=src[:, 1])
-            if h == 0:
-                nc.vector.tensor_copy(
-                    out=w2_scale_dealt[:].rearrange("p (t g i) -> p g t i", t=PACK, i=16),
-                    in_=w2_scale_raw[:].rearrange("p (g i t) -> p g t i", t=PACK, i=16),
-                )
+        early = w1_early[:].rearrange("p j (m e u) -> p u m j e", e=2, u=2)
+        late = w1_late[:].rearrange("p (m e u) -> p u m e", e=2, u=2)
+        nc.vector.tensor_copy(out=w1_grouped[0][:, :, :, : PACK - 1].rearrange("p e m j -> p m j e"), in_=early[:, 0])
+        nc.scalar.copy(out=w1_grouped[1][:, :, :, : PACK - 1].rearrange("p e m j -> p m j e"), in_=early[:, 1])
+        for e in range(2):
+            nc.vector.tensor_copy(out=w1_grouped[0][:, e, :, PACK - 1], in_=late[:, 0, :, e])
+        nc.scalar.copy(out=w1_grouped[1][:, :, :, PACK - 1].rearrange("p e m -> p m e"), in_=late[:, 1])
 
-        z = [keep.tile([P, S], F32, name="z%d" % t, tag="z%d" % t, align_bytes=64) for t in range(PACK)]
-
-        banks = {}
-
-        def project(slot, t):
-            nc.vector.quantize_mx(
-                out=w1_codes[t][:].bitcast(FP8X4),
-                scales=w1_scale[t][:],
-                in_=w1_grouped[t % 2][:, t // 2].rearrange("p m j -> p (m j)"),
-            )
-            width = (CHUNK, HALF, S, S)[slot]
+        banks = []
+        for slot, t in enumerate(PLANE_ORDER):
+            quantize(nc, w1_codes[t][:], w1_scale[t][:], w1_grouped[t % 2][:, t // 2])
+            width = (CHUNK, 2 * CHUNK, S, S)[slot]
+            banks.append([])
             for first in range(0, S, width):
                 cols = slice(first, first + width)
-                acc = psum.tile([P, width], F32, name="acc", tag="bank")
-                nc.tensor.matmul_mx(
-                    out=acc[:],
-                    lhsT=w1_codes[t][:].bitcast(FP8X4),
-                    lhsT_scale=w1_scale[t][:],
-                    rhs=x_word_picked[:, cols].bitcast(FP8X4),
-                    rhs_scale=x_scale_picked[:, cols],
-                    start=True,
-                    stop=True,
-                )
-                banks.setdefault(t, []).append((cols, acc))
+                acc = psum.tile([P, width], F32, name="acc", tag="bank%d" % ((0, 1, 2, 3), (3, 2), (3,), (2,))[slot][first // width])
+                product(nc, acc[:], w1_codes[t][:], w1_scale[t][:], x_word_picked[:, cols], x_scale_picked[:, cols])
+                banks[slot].append((cols, acc))
 
-        y, a, b, minus_b = {}, {}, {}, {}
-        y_offset = (9280, 2048, 4032, 6016)
-        minus_b_offset = {0: 1088, 2: 6208}
-        z_grouped_offset = (4160, 7232)
+        z = [tile("z%d" % slot, [P, S], F32) for slot in range(PACK)]
+        a = tiles("a", PACK, [P, V], F32)
+        b = tiles("b", PACK, [P, V], F32)
+        y, minus_b = {}, {}
+        whole, low, high = slice(0, V), slice(0, V // 2), slice(V // 2, V)
+        grouped_bytes = S * PACK * 2
 
-        def fetch(slot):
-            t = PLANE_ORDER[slot]
-            y[t] = ring.tile([P, S], F32, name="y%d" % t, align_bytes=64, offset=y_offset[slot])
-            for cols, acc in banks[t]:
-                nc.scalar.activation(out=y[t][:, cols], in_=acc[:], func=COPY, scale=0.75)
-            a[t] = keep.tile([P, V], F32, name="a%d" % t, align_bytes=64)
-            nc.scalar.activation(out=a[t][:], in_=y[t][:].indirect(la_sb[:]), func=COPY)
-            b[t] = keep.tile([P, V], F32, name="b%d" % t, align_bytes=64)
-            if slot == 0:
-                nc.vector.tensor_copy(out=b[t][:], in_=y[t][:].indirect(lb_sb[:]))
+        def entries(lists, part):
+            return lists[:, part.start // LIST : part.stop // LIST]
+
+        def empty(slot):
+            if slot < PACK - 1:
+                y[slot] = tile("y%d" % slot, [P, S], F32)
             else:
-                nc.scalar.activation(out=b[t][:], in_=y[t][:].indirect(lb_sb[:]), func=COPY)
+                y[slot] = reuse.tile([P, S], F32, name="y%d" % slot, align_bytes=64, offset=grouped_bytes - 512)
+            for cols, acc in banks[slot]:
+                nc.scalar.activation(out=y[slot][:, cols], in_=acc[:], func=COPY, scale=0.75)
 
-        def put_sum(slot):
-            t = PLANE_ORDER[slot]
-            nc.vector.tensor_tensor(z[t][:].indirect(la_sb[:]), a[t][:], b[t][:], ADD)
+        def fetch(slot, part):
+            nc.scalar.activation(out=a[slot][:, part], in_=y[slot][:].indirect(entries(la_sb, part)), func=COPY)
+            if slot == 0:
+                nc.vector.tensor_copy(out=b[slot][:, part], in_=y[slot][:].indirect(entries(lb_sb, part)))
+            else:
+                nc.scalar.activation(out=b[slot][:, part], in_=y[slot][:].indirect(entries(lb_sb, part)), func=COPY)
+
+        def put_sum(slot, part):
+            nc.vector.tensor_tensor(z[slot][:].indirect(entries(la_sb, part)), a[slot][:, part], b[slot][:, part], ADD)
 
         def negate(slot):
-            t = PLANE_ORDER[slot]
-            if slot in minus_b_offset:
-                minus_b[t] = ring.tile([P, V], F32, name="minus_b%d" % t, align_bytes=64, offset=minus_b_offset[slot])
+            if slot == 2:
+                minus_b[slot] = reuse.tile([P, V], F32, name="minus_b2", align_bytes=64, offset=grouped_bytes)
             else:
-                tag = "z%d" % PLANE_ORDER[0] if slot == PACK - 1 else "minus_b%d" % t
-                minus_b[t] = keep.tile([P, V], F32, name="minus_b%d" % t, tag=tag, align_bytes=64)
-            nc.scalar.activation(out=minus_b[t][:], in_=b[t][:], func=COPY, scale=-1.0)
+                tag = ("w1_codes%d" % PLANE_ORDER[2], "y2", None, "z0")[slot]
+                minus_b[slot] = tile("minus_b%d" % slot, [P, V], F32, tag=tag)
+            nc.scalar.activation(out=minus_b[slot][:], in_=b[slot][:], func=COPY, scale=-1.0)
 
         def put_difference(slot):
-            t = PLANE_ORDER[slot]
-            nc.vector.tensor_tensor(z[t][:].indirect(lb_sb[:]), a[t][:], minus_b[t][:], ADD)
+            nc.vector.tensor_tensor(z[slot][:].indirect(lb_sb[:]), a[slot][:], minus_b[slot][:], ADD)
 
-        def regroup(slot):
-            t = PLANE_ORDER[slot]
-            for h in range(2):
-                if slot < PACK - 1:
-                    nc.scalar.copy(out=z_grouped[h][:, :, t], in_=z[t][:, h * HALF : (h + 1) * HALF])
-                else:
-                    engine_copy = nc.vector.tensor_copy if h == 0 else nc.scalar.copy
-                    for first in range(0, HALF, CHUNK):
-                        engine_copy(
-                            out=z_grouped[h][:, first : first + CHUNK, t],
-                            in_=z[t][:, h * HALF + first : h * HALF + first + CHUNK],
-                        )
+        def regroup(copy, slot, first, width):
+            cols = slice(first, first + width)
+            copy(out=z_grouped[:, cols, PLANE_ORDER[slot]], in_=z[slot][:, cols])
 
-        for slot, t in enumerate(PLANE_ORDER):
-            project(slot, t)
-        for slot in (0, 1):
-            fetch(slot)
-            put_sum(slot)
-        for slot in (0, 1):
-            negate(slot)
-            put_difference(slot)
-        for slot in (2, 3):
-            fetch(slot)
-            put_sum(slot)
+        empty(0)
+        fetch(0, whole)
+        put_sum(0, whole)
+        empty(1)
+        fetch(1, low)
+        put_sum(1, low)
+        negate(0)
+        put_difference(0)
+        fetch(1, high)
+        put_sum(1, high)
+        empty(2)
+        fetch(2, whole)
+        put_sum(2, whole)
+        negate(1)
+        put_difference(1)
+        empty(3)
+        fetch(3, whole)
+        put_sum(3, whole)
         negate(2)
         put_difference(2)
-        w2_codes = ring.tile([P, N], U32, name="w2_codes", align_bytes=64, offset=2112)
-        dealt = w2_codes[:].rearrange("p (t g i) -> p g t i", t=PACK, i=LINE)
-        raw = w2_word_raw[:].rearrange("p (g i t) -> p g t i", t=PACK, i=LINE)
-        for first in range(0, P // LINE, 8):
-            nc.scalar.copy(out=dealt[:, first : first + 8], in_=raw[:, first : first + 8])
-        z_grouped = [
-            ring.tile([P, HALF, PACK], BF16, name="z_grouped%d" % h, align_bytes=64, offset=z_grouped_offset[h]) for h in range(2)
-        ]
-        regroup(0)
+
+        w2_codes = reuse.tile([P, N], U32, name="w2_codes", align_bytes=64, offset=grouped_bytes + 1024)
+        nc.scalar.copy(
+            out=w2_codes[:].rearrange("p (t g i) -> p g t i", t=PACK, i=LINE),
+            in_=w2_word_raw[:].rearrange("p (g i t) -> p g t i", t=PACK, i=LINE),
+        )
+        z_grouped = reuse.tile([P, S, PACK], BF16, name="z_grouped", align_bytes=64, offset=0)
+        regroup(nc.scalar.copy, 0, 0, S)
         negate(PACK - 1)
         put_difference(PACK - 1)
-        for slot in range(1, PACK):
-            regroup(slot)
-
-        w2_scale = [w2_scale_dealt[:, t * P : (t + 1) * P] for t in range(PACK)]
+        regroup(nc.scalar.copy, 1, 0, S)
+        for h in range(2):
+            regroup(nc.scalar.copy, 2, h * S // 2, S // 2)
+        for c in range(CHUNKS):
+            regroup(nc.vector.tensor_copy if c < 2 else nc.scalar.copy, PACK - 1, c * CHUNK, CHUNK)
 
         z_codes = tiles("z_codes", CHUNKS, [P, CHUNK], U32)
         z_scale = tiles("z_scale", CHUNKS, [P, CHUNK], U8)
         result = tiles("result", CHUNKS, [P, PACK, CHUNK], F32)
         result_grouped = tiles("result_grouped", CHUNKS, [P, CHUNK, PACK], BF16)
-        out_codes = keep.tile([P, S], U32, name="out_codes", align_bytes=64)
-        out_scale = keep.tile([P, S], U8, name="out_scale", align_bytes=64)
+        out_codes = tile("out_codes", [P, S], U32)
+        out_scale = tile("out_scale", [P, S], U8)
         out_rows = out_0.rearrange("(p t) n -> p t n", t=PACK)
         out_words = out_1[0].rearrange("p n t -> p (n t)").bitcast(I32)
 
         for c in range(CHUNKS):
-            nc.vector.quantize_mx(
-                out=z_codes[c][:].bitcast(FP8X4),
-                scales=z_scale[c][:],
-                in_=z_grouped[c // 2][:, (c % 2) * CHUNK : (c % 2 + 1) * CHUNK, :].rearrange("p n t -> p (n t)"),
-            )
+            quantize(nc, z_codes[c][:], z_scale[c][:], z_grouped[:, c * CHUNK : (c + 1) * CHUNK, :])
         for c in range(CHUNKS):
             cols = slice(c * CHUNK, (c + 1) * CHUNK)
             for first in range(0, PACK, 2):
-                planes = slice(first, first + 2)
-                acc = psum.tile([P, 2, CHUNK], F32, name="acc", tag="bank")
+                acc = psum.tile([P, 2, CHUNK], F32, name="acc", tag="bank%d" % ((4 + 2 * c + first // 2) % 8))
                 for t in range(first, first + 2):
-                    nc.tensor.matmul_mx(
-                        out=acc[:, t - first, :],
-                        lhsT=w2_codes[:, t * P : (t + 1) * P].bitcast(FP8X4),
-                        lhsT_scale=w2_scale[t],
-                        rhs=z_codes[c][:].bitcast(FP8X4),
-                        rhs_scale=z_scale[c][:],
-                        start=True,
-                        stop=True,
-                    )
-                nc.scalar.copy(out=result[c][:, planes, :], in_=acc[:])
+                    w_cols = slice(t * P, (t + 1) * P)
+                    product(nc, acc[:, t - first, :], w2_codes[:, w_cols], w2_scale[:, w_cols], z_codes[c][:], z_scale[c][:])
+                nc.scalar.copy(out=result[c][:, first : first + 2, :], in_=acc[:])
             nc.sync.dma_start(out=out_rows[:, :, cols], in_=result[c][:])
             nc.vector.tensor_copy(
                 out=result_grouped[c][:].rearrange("p (g i) t -> p g t i", i=LINE),
                 in_=result[c][:].rearrange("p t (g i) -> p g t i", i=LINE),
             )
-            nc.vector.quantize_mx(
-                out=out_codes[:, cols].bitcast(FP8X4),
-                scales=out_scale[:, cols],
-                in_=result_grouped[c][:].rearrange("p n t -> p (n t)"),
-            )
+            quantize(nc, out_codes[:, cols], out_scale[:, cols], result_grouped[c][:])
             if c == CHUNKS - 2:
                 nc.sync.dma_start(out=out_words[:, : (c + 1) * CHUNK], in_=out_codes[:, : (c + 1) * CHUNK].bitcast(I32))
             if c == CHUNKS - 1:
                 nc.scalar.dma_start(out=out_words[:, cols], in_=out_codes[:, cols].bitcast(I32))
         for q in range(QUADS):
             queue = nc.sync if q % 2 == 0 else nc.scalar
-            queue.dma_start(
-                out=out_2[0][4 * q : 4 * q + 4, :].bitcast(I32),
-                in_=out_scale[32 * q : 32 * q + 4, :].bitcast(I32),
-            )
+            queue.dma_start(out=out_2[0][4 * q : 4 * q + 4, :].bitcast(I32), in_=out_scale[32 * q : 32 * q + 4, :].bitcast(I32))

@@ -45,7 +45,6 @@ def tile_picked_haarinp_none_po_kernel(tc, x_words, x_scales, w1, w2_words, w2_s
     nc = tc.nc
     with ExitStack() as ctx:
         keep = ctx.enter_context(tc.tile_pool(name="keep", bufs=1))
-        reuse = ctx.enter_context(tc.tile_pool(name="reuse", bufs=1))
         psum = ctx.enter_context(tc.psum_pool(name="psum", bufs=1))
 
         def tile(name, shape, dtype, tag=None):
@@ -106,34 +105,29 @@ def tile_picked_haarinp_none_po_kernel(tc, x_words, x_scales, w1, w2_words, w2_s
             nc.vector.tensor_copy(out=w1_grouped[0][:, e, :, PACK - 1], in_=late[:, 0, :, e])
         nc.scalar.copy(out=w1_grouped[1][:, :, :, PACK - 1].rearrange("p e m -> p m e"), in_=late[:, 1])
 
-        banks = []
-        for slot, t in enumerate(PLANE_ORDER):
+        for t in PLANE_ORDER:
             quantize(nc, w1_codes[t][:], w1_scale[t][:], w1_grouped[t % 2][:, t // 2])
-            width = (CHUNK, 2 * CHUNK, S, S)[slot]
-            banks.append([])
-            for first in range(0, S, width):
-                cols = slice(first, first + width)
-                acc = psum.tile([P, width], F32, name="acc", tag="bank%d" % ((0, 1, 2, 3), (3, 2), (3,), (2,))[slot][first // width])
-                product(nc, acc[:], w1_codes[t][:], w1_scale[t][:], x_word_picked[:, cols], x_scale_picked[:, cols])
-                banks[slot].append((cols, acc))
 
         z = [tile("z%d" % slot, [P, S], F32) for slot in range(PACK)]
         a = tiles("a", PACK, [P, V], F32)
         b = tiles("b", PACK, [P, V], F32)
-        y, minus_b = {}, {}
+        y = tiles("y", PACK, [P, S], F32)
+        minus_b = {}
         whole, low, high = slice(0, V), slice(0, V // 2), slice(V // 2, V)
-        grouped_bytes = S * PACK * 2
+        left, right = slice(0, S // 2), slice(S // 2, S)
+
+        def bank(index, width):
+            return psum.tile([P, width], F32, name="acc", tag="bank%d" % index)
+
+        def project(slot, cols, acc):
+            t = PLANE_ORDER[slot]
+            product(nc, acc, w1_codes[t][:], w1_scale[t][:], x_word_picked[:, cols], x_scale_picked[:, cols])
+
+        def empty(slot, cols, acc):
+            nc.scalar.activation(out=y[slot][:, cols], in_=acc, func=COPY, scale=0.75)
 
         def entries(lists, part):
             return lists[:, part.start // LIST : part.stop // LIST]
-
-        def empty(slot):
-            if slot < PACK - 1:
-                y[slot] = tile("y%d" % slot, [P, S], F32)
-            else:
-                y[slot] = reuse.tile([P, S], F32, name="y%d" % slot, align_bytes=64, offset=grouped_bytes - 512)
-            for cols, acc in banks[slot]:
-                nc.scalar.activation(out=y[slot][:, cols], in_=acc[:], func=COPY, scale=0.75)
 
         def fetch(slot, part):
             nc.scalar.activation(out=a[slot][:, part], in_=y[slot][:].indirect(entries(la_sb, part)), func=COPY)
@@ -146,55 +140,66 @@ def tile_picked_haarinp_none_po_kernel(tc, x_words, x_scales, w1, w2_words, w2_s
             nc.vector.tensor_tensor(z[slot][:].indirect(entries(la_sb, part)), a[slot][:, part], b[slot][:, part], ADD)
 
         def negate(slot):
-            if slot == 2:
-                minus_b[slot] = reuse.tile([P, V], F32, name="minus_b2", align_bytes=64, offset=grouped_bytes)
-            else:
-                tag = ("w1_codes%d" % PLANE_ORDER[2], "y2", None, "z0")[slot]
-                minus_b[slot] = tile("minus_b%d" % slot, [P, V], F32, tag=tag)
+            minus_b[slot] = tile("minus_b%d" % slot, [P, V], F32, tag="z0" if slot == PACK - 1 else None)
             nc.scalar.activation(out=minus_b[slot][:], in_=b[slot][:], func=COPY, scale=-1.0)
 
         def put_difference(slot):
             nc.vector.tensor_tensor(z[slot][:].indirect(lb_sb[:]), a[slot][:], minus_b[slot][:], ADD)
 
-        def regroup(copy, slot, first, width):
-            cols = slice(first, first + width)
+        def regroup(copy, slot, cols):
             copy(out=z_grouped[:, cols, PLANE_ORDER[slot]], in_=z[slot][:, cols])
 
-        empty(0)
+        for c in range(CHUNKS):
+            cols = slice(c * CHUNK, (c + 1) * CHUNK)
+            acc = bank(c, CHUNK)
+            project(0, cols, acc[:])
+            empty(0, cols, acc[:])
         fetch(0, whole)
         put_sum(0, whole)
-        empty(1)
+        both = bank(2, S)
+        project(1, left, both[:, left])
+        project(2, left, both[:, right])
+        acc = bank(3, S // 2)
+        project(1, right, acc[:])
+        empty(1, left, both[:, left])
+        empty(1, right, acc[:])
         fetch(1, low)
         put_sum(1, low)
+        empty(2, left, both[:, right])
         negate(0)
         put_difference(0)
+        acc = bank(3, S // 2)
+        project(2, right, acc[:])
+        empty(2, right, acc[:])
         fetch(1, high)
         put_sum(1, high)
-        empty(2)
         fetch(2, whole)
         put_sum(2, whole)
+        acc = bank(2, S)
+        project(3, slice(0, S), acc[:])
+        empty(3, slice(0, S), acc[:])
+        fetch(3, whole)
         negate(1)
         put_difference(1)
-        empty(3)
-        fetch(3, whole)
         put_sum(3, whole)
         negate(2)
         put_difference(2)
 
-        w2_codes = reuse.tile([P, N], U32, name="w2_codes", align_bytes=64, offset=grouped_bytes + 1024)
+        z_grouped = tile("z_grouped", [P, S, PACK], BF16, tag="y2")
+        for half in (left, right):
+            regroup(nc.scalar.copy, 0, half)
+        negate(PACK - 1)
+        put_difference(PACK - 1)
+        w2_codes = tile("w2_codes", [P, N], U32, tag="y1")
         nc.scalar.copy(
             out=w2_codes[:].rearrange("p (t g i) -> p g t i", t=PACK, i=LINE),
             in_=w2_word_raw[:].rearrange("p (g i t) -> p g t i", t=PACK, i=LINE),
         )
-        z_grouped = reuse.tile([P, S, PACK], BF16, name="z_grouped", align_bytes=64, offset=0)
-        regroup(nc.scalar.copy, 0, 0, S)
-        negate(PACK - 1)
-        put_difference(PACK - 1)
-        regroup(nc.scalar.copy, 1, 0, S)
-        for h in range(2):
-            regroup(nc.scalar.copy, 2, h * S // 2, S // 2)
+        for slot in (1, 2):
+            for half in (left, right):
+                regroup(nc.scalar.copy, slot, half)
         for c in range(CHUNKS):
-            regroup(nc.vector.tensor_copy if c < 2 else nc.scalar.copy, PACK - 1, c * CHUNK, CHUNK)
+            regroup(nc.vector.tensor_copy if c < 2 else nc.scalar.copy, PACK - 1, slice(c * CHUNK, (c + 1) * CHUNK))
 
         z_codes = tiles("z_codes", CHUNKS, [P, CHUNK], U32)
         z_scale = tiles("z_scale", CHUNKS, [P, CHUNK], U8)

@@ -154,28 +154,31 @@ def tile_picked_haarinp_none_po_kernel(tc, x_words, x_scales, w1, w2_words, w2_s
             acc = bank(c, CHUNK)
             project(0, cols, acc[:])
             empty(0, cols, acc[:])
+        for c in range(2):
+            cols = slice(c * CHUNK, (c + 1) * CHUNK)
+            acc = bank(4 + c, CHUNK)
+            project(1, cols, acc[:])
+            nc.vector.tensor_scalar_mul(y[1][:, cols], acc[:], 0.75)
         fetch(0, whole)
         put_sum(0, whole)
-        both = bank(2, S)
-        project(1, left, both[:, left])
-        project(2, left, both[:, right])
-        acc = bank(3, S // 2)
+        acc = bank(2, S // 2)
         project(1, right, acc[:])
-        empty(1, left, both[:, left])
         empty(1, right, acc[:])
         fetch(1, low)
         put_sum(1, low)
-        empty(2, left, both[:, right])
+        acc = bank(3, S // 2)
+        project(2, left, acc[:])
+        empty(2, left, acc[:])
         negate(0)
         put_difference(0)
-        acc = bank(3, S // 2)
+        acc = bank(2, S // 2)
         project(2, right, acc[:])
         empty(2, right, acc[:])
         fetch(1, high)
         put_sum(1, high)
         fetch(2, whole)
         put_sum(2, whole)
-        acc = bank(2, S)
+        acc = bank(3, S)
         project(3, slice(0, S), acc[:])
         empty(3, slice(0, S), acc[:])
         fetch(3, whole)
@@ -215,7 +218,7 @@ def tile_picked_haarinp_none_po_kernel(tc, x_words, x_scales, w1, w2_words, w2_s
         for c in range(CHUNKS):
             cols = slice(c * CHUNK, (c + 1) * CHUNK)
             for first in range(0, PACK, 2):
-                acc = psum.tile([P, 2, CHUNK], F32, name="acc", tag="bank%d" % ((4 + 2 * c + first // 2) % 8))
+                acc = psum.tile([P, 2, CHUNK], F32, name="acc", tag="bank%d" % ((6 + 2 * c + first // 2) % 8))
                 for t in range(first, first + 2):
                     w_cols = slice(t * P, (t + 1) * P)
                     product(nc, acc[:, t - first, :], w2_codes[:, w_cols], w2_scale[:, w_cols], z_codes[c][:], z_scale[c][:])

@@ -229,10 +229,7 @@ def tile_picked_haarinp_none_po_kernel(tc, x_words, x_scales, w1, w2_words, w2_s
                 in_=result[c][:].rearrange("p t (g i) -> p g t i", i=LINE),
             )
             quantize(nc, out_codes[:, cols], out_scale[:, cols], result_grouped[c][:])
-            if c == CHUNKS - 2:
-                nc.sync.dma_start(out=out_words[:, : (c + 1) * CHUNK], in_=out_codes[:, : (c + 1) * CHUNK].bitcast(I32))
-            if c == CHUNKS - 1:
-                nc.scalar.dma_start(out=out_words[:, cols], in_=out_codes[:, cols].bitcast(I32))
+        nc.sync.dma_start(out=out_words, in_=out_codes[:].bitcast(I32))
         for q in range(QUADS):
             queue = nc.sync if q % 2 == 0 else nc.scalar
             queue.dma_start(out=out_2[0][4 * q : 4 * q + 4, :].bitcast(I32), in_=out_scale[32 * q : 32 * q + 4, :].bitcast(I32))

@@ -74,7 +74,7 @@ def tile_picked_haarinp_none_po_kernel(tc, x_words, x_scales, w1, w2_words, w2_s
         nc.vector.memset(w2_scale[:].bitcast(I32), 0)
 
         w1_rows = w1.rearrange("(p j) c -> p j c", j=PACK)
-        nc.sync.dma_start(out=x_scale_table[16:32, :].bitcast(I32), in_=x_scales[0].bitcast(I32))
+        nc.scalar.dma_start(out=x_scale_table[16:32, :].bitcast(I32), in_=x_scales[0].bitcast(I32))
         nc.sync.dma_start(offs_sb[:], offs)
         nc.sync.dma_start(out=x_word_table[:].bitcast(I32), in_=x_words[0].rearrange("p n t -> p (n t)").bitcast(I32))
         nc.sync.dma_start(out=w2_scale_raw[0:16, :].bitcast(I32), in_=w2_scales[0].bitcast(I32))

@@ -80,11 +80,11 @@ def tile_picked_haarinp_none_po_kernel(tc, x_words, x_scales, w1, w2_words, w2_s
         nc.sync.dma_start(out=w2_scale_raw[0:16, :].bitcast(I32), in_=w2_scales[0].bitcast(I32))
         nc.sync.dma_start(out=w1_early[:], in_=w1_rows[:, : PACK - 1, :])
         nc.sync.dma_start(out=w1_late[:], in_=w1_rows[:, PACK - 1, :])
-        nc.sync.dma_start(la_sb[:], la)
-        nc.sync.dma_start(lb_sb[:], lb)
 
         nc.vector.tensor_copy(out=x_scale_gathered[:], in_=x_scale_table[:].indirect(offs_sb[:]))
         move_scale_rows(nc, x_scale_picked, x_scale_gathered, 16)
+        nc.sync.dma_start(la_sb[:], la)
+        nc.sync.dma_start(lb_sb[:], lb)
         w2_word_raw = tile("w2_word_raw", [P, N], U32, tag="x_scale_table")
         nc.sync.dma_start(out=w2_word_raw[:].bitcast(I32), in_=w2_words[0].rearrange("p n t -> p (n t)").bitcast(I32))
         nc.vector.tensor_copy(out=x_word_picked[:], in_=x_word_table[:].indirect(offs_sb[:]))

@@ -204,9 +204,11 @@ def tile_picked_haarinp_none_po_kernel(tc, x_words, x_scales, w1, w2_words, w2_s
         for c in range(CHUNKS):
             regroup(nc.vector.tensor_copy if c < 2 else nc.scalar.copy, PACK - 1, slice(c * CHUNK, (c + 1) * CHUNK))
 
+        chunk_cols = [slice(c * CHUNK, (c + 1) * CHUNK) for c in range(CHUNKS)]
+        halves = (left, right)
         z_codes = tiles("z_codes", CHUNKS, [P, CHUNK], U32)
         z_scale = tiles("z_scale", CHUNKS, [P, CHUNK], U8)
-        result = tiles("result", CHUNKS, [P, PACK, CHUNK], F32)
+        result = tiles("result", 2, [P, PACK, S // 2], F32)
         result_grouped = tiles("result_grouped", CHUNKS, [P, CHUNK, PACK], BF16)
         out_codes = tile("out_codes", [P, S], U32)
         out_scale = tile("out_scale", [P, S], U8)
@@ -214,21 +216,23 @@ def tile_picked_haarinp_none_po_kernel(tc, x_words, x_scales, w1, w2_words, w2_s
         out_words = out_1[0].rearrange("p n t -> p (n t)").bitcast(I32)
 
         for c in range(CHUNKS):
-            quantize(nc, z_codes[c][:], z_scale[c][:], z_grouped[:, c * CHUNK : (c + 1) * CHUNK, :])
-        for c in range(CHUNKS):
-            cols = slice(c * CHUNK, (c + 1) * CHUNK)
+            quantize(nc, z_codes[c][:], z_scale[c][:], z_grouped[:, chunk_cols[c], :])
+        for h in range(2):
             for first in range(0, PACK, 2):
-                acc = psum.tile([P, 2, CHUNK], F32, name="acc", tag="bank%d" % ((6 + 2 * c + first // 2) % 8))
-                for t in range(first, first + 2):
-                    w_cols = slice(t * P, (t + 1) * P)
-                    product(nc, acc[:, t - first, :], w2_codes[:, w_cols], w2_scale[:, w_cols], z_codes[c][:], z_scale[c][:])
-                nc.scalar.copy(out=result[c][:, first : first + 2, :], in_=acc[:])
-            nc.sync.dma_start(out=out_rows[:, :, cols], in_=result[c][:])
-            nc.vector.tensor_copy(
-                out=result_grouped[c][:].rearrange("p (g i) t -> p g t i", i=LINE),
-                in_=result[c][:].rearrange("p t (g i) -> p g t i", i=LINE),
-            )
-            quantize(nc, out_codes[:, cols], out_scale[:, cols], result_grouped[c][:])
+                for k in range(2):
+                    c = 2 * h + k
+                    acc = psum.tile([P, 2, CHUNK], F32, name="acc", tag="bank%d" % ((6 + 4 * h + first + k) % 8))
+                    for t in range(first, first + 2):
+                        w_cols = slice(t * P, (t + 1) * P)
+                        product(nc, acc[:, t - first, :], w2_codes[:, w_cols], w2_scale[:, w_cols], z_codes[c][:], z_scale[c][:])
+                    nc.scalar.copy(out=result[h][:, first : first + 2, chunk_cols[k]], in_=acc[:])
+                    if first > 0:
+                        nc.vector.tensor_copy(
+                            out=result_grouped[c][:].rearrange("p (g i) t -> p g t i", i=LINE),
+                            in_=result[h][:, :, chunk_cols[k]].rearrange("p t (g i) -> p g t i", i=LINE),
+                        )
+                        quantize(nc, out_codes[:, chunk_cols[c]], out_scale[:, chunk_cols[c]], result_grouped[c][:])
+                nc.sync.dma_start(out=out_rows[:, first : first + 2, halves[h]], in_=result[h][:, first : first + 2, :])
         nc.sync.dma_start(out=out_words, in_=out_codes[:].bitcast(I32))
         for q in range(QUADS):
             queue = nc.sync if q % 2 == 0 else nc.scalar

@@ -13,6 +13,8 @@ U8 = mybir.dt.uint8
 FP8X4 = mybir.dt.float8_e4m3fn_x4
 COPY = mybir.ActivationFunctionType.Copy
 ADD = mybir.AluOpType.add
+SUB = mybir.AluOpType.subtract
+MULT = mybir.AluOpType.mult
 
 P = 128
 PACK = 4
@@ -21,7 +23,6 @@ CHUNK = 128
 CHUNKS = S // CHUNK
 LINE = 4
 LIST = 16
-PLANE_ORDER = (0, 2, 3, 1)
 
 FLOPS = 2 * K * H * S + 2 * H * N * S
 
@@ -80,11 +81,11 @@ def tile_picked_haarinp_none_po_kernel(tc, x_words, x_scales, w1, w2_words, w2_s
         nc.sync.dma_start(out=w2_scale_raw[0:16, :].bitcast(I32), in_=w2_scales[0].bitcast(I32))
         nc.sync.dma_start(out=w1_early[:], in_=w1_rows[:, : PACK - 1, :])
         nc.sync.dma_start(out=w1_late[:], in_=w1_rows[:, PACK - 1, :])
+        nc.sync.dma_start(la_sb[:], la)
+        nc.sync.dma_start(lb_sb[:], lb)
 
         nc.vector.tensor_copy(out=x_scale_gathered[:], in_=x_scale_table[:].indirect(offs_sb[:]))
         move_scale_rows(nc, x_scale_picked, x_scale_gathered, 16)
-        nc.sync.dma_start(la_sb[:], la)
-        nc.sync.dma_start(lb_sb[:], lb)
         w2_word_raw = tile("w2_word_raw", [P, N], U32, tag="x_scale_table")
         nc.sync.dma_start(out=w2_word_raw[:].bitcast(I32), in_=w2_words[0].rearrange("p n t -> p (n t)").bitcast(I32))
         nc.vector.tensor_copy(out=x_word_picked[:], in_=x_word_table[:].indirect(offs_sb[:]))
@@ -97,115 +98,101 @@ def tile_picked_haarinp_none_po_kernel(tc, x_words, x_scales, w1, w2_words, w2_s
         w1_grouped = tiles("w1_grouped", 2, [P, 2, P, PACK], BF16)
         w1_codes = tiles("w1_codes", PACK, [P, P], U32)
         w1_scale = tiles("w1_scale", PACK, [P, P], U8)
-        early = w1_early[:].rearrange("p j (m e u) -> p u m j e", e=2, u=2)
-        late = w1_late[:].rearrange("p (m e u) -> p u m e", e=2, u=2)
+        early = w1_early[:].rearrange("p j (m u e) -> p u m j e", e=2, u=2)
+        late = w1_late[:].rearrange("p (m u e) -> p u m e", e=2, u=2)
         nc.vector.tensor_copy(out=w1_grouped[0][:, :, :, : PACK - 1].rearrange("p e m j -> p m j e"), in_=early[:, 0])
         nc.scalar.copy(out=w1_grouped[1][:, :, :, : PACK - 1].rearrange("p e m j -> p m j e"), in_=early[:, 1])
         for e in range(2):
             nc.vector.tensor_copy(out=w1_grouped[0][:, e, :, PACK - 1], in_=late[:, 0, :, e])
         nc.scalar.copy(out=w1_grouped[1][:, :, :, PACK - 1].rearrange("p e m -> p m e"), in_=late[:, 1])
 
-        for t in PLANE_ORDER:
-            quantize(nc, w1_codes[t][:], w1_scale[t][:], w1_grouped[t % 2][:, t // 2])
+        for t in range(PACK):
+            quantize(nc, w1_codes[t][:], w1_scale[t][:], w1_grouped[t // 2][:, t % 2])
 
-        z = [tile("z%d" % slot, [P, S], F32) for slot in range(PACK)]
-        a = tiles("a", PACK, [P, V], F32)
-        b = tiles("b", PACK, [P, V], F32)
         y = tiles("y", PACK, [P, S], F32)
-        minus_b = {}
-        whole, low, high = slice(0, V), slice(0, V // 2), slice(V // 2, V)
+        a = tiles("a", PACK, [P, V], F32)
+        b = tiles("b", PACK - 1, [P, V], F32)
+        sm = tiles("sm", PACK, [P, V], F32)
+        df = {t: tile("df%d" % t, [P, V], F32) for t in (0, 2, 3)}
+        z = tiles("z", PACK, [P, S], F32)
         left, right = slice(0, S // 2), slice(S // 2, S)
 
-        def bank(index, width):
-            return psum.tile([P, width], F32, name="acc", tag="bank%d" % index)
-
-        def project(slot, cols, acc):
-            t = PLANE_ORDER[slot]
-            product(nc, acc, w1_codes[t][:], w1_scale[t][:], x_word_picked[:, cols], x_scale_picked[:, cols])
-
-        def empty(slot, cols, acc):
-            nc.scalar.activation(out=y[slot][:, cols], in_=acc, func=COPY, scale=0.75)
-
-        def entries(lists, part):
-            return lists[:, part.start // LIST : part.stop // LIST]
-
-        def fetch(slot, part):
-            nc.scalar.activation(out=a[slot][:, part], in_=y[slot][:].indirect(entries(la_sb, part)), func=COPY)
-            if slot == 0:
-                nc.vector.tensor_copy(out=b[slot][:, part], in_=y[slot][:].indirect(entries(lb_sb, part)))
+        def project(t, cols, bank, on_vector):
+            acc = psum.tile([P, cols.stop - cols.start], F32, name="acc", tag="bank%d" % bank)
+            product(nc, acc[:], w1_codes[t][:], w1_scale[t][:], x_word_picked[:, cols], x_scale_picked[:, cols])
+            if on_vector:
+                nc.vector.tensor_scalar_mul(y[t][:, cols], acc[:], 0.75)
             else:
-                nc.scalar.activation(out=b[slot][:, part], in_=y[slot][:].indirect(entries(lb_sb, part)), func=COPY)
+                nc.scalar.activation(out=y[t][:, cols], in_=acc[:], func=COPY, scale=0.75)
 
-        def put_sum(slot, part):
-            nc.vector.tensor_tensor(z[slot][:].indirect(entries(la_sb, part)), a[slot][:, part], b[slot][:, part], ADD)
-
-        def negate(slot):
-            minus_b[slot] = tile("minus_b%d" % slot, [P, V], F32, tag="z0" if slot == PACK - 1 else None)
-            nc.scalar.activation(out=minus_b[slot][:], in_=b[slot][:], func=COPY, scale=-1.0)
-
-        def put_difference(slot):
-            nc.vector.tensor_tensor(z[slot][:].indirect(lb_sb[:]), a[slot][:], minus_b[slot][:], ADD)
-
-        def regroup(copy, slot, cols):
-            copy(out=z_grouped[:, cols, PLANE_ORDER[slot]], in_=z[slot][:, cols])
+        def move(out, in_, on_vector):
+            if on_vector:
+                nc.vector.tensor_copy(out=out, in_=in_)
+            else:
+                nc.scalar.activation(out=out, in_=in_, func=COPY)
 
         for c in range(CHUNKS):
-            cols = slice(c * CHUNK, (c + 1) * CHUNK)
-            acc = bank(c, CHUNK)
-            project(0, cols, acc[:])
-            empty(0, cols, acc[:])
-        for c in range(2):
-            cols = slice(c * CHUNK, (c + 1) * CHUNK)
-            acc = bank(4 + c, CHUNK)
-            project(1, cols, acc[:])
-            nc.vector.tensor_scalar_mul(y[1][:, cols], acc[:], 0.75)
-        fetch(0, whole)
-        put_sum(0, whole)
-        acc = bank(2, S // 2)
-        project(1, right, acc[:])
-        empty(1, right, acc[:])
-        fetch(1, low)
-        put_sum(1, low)
-        acc = bank(3, S // 2)
-        project(2, left, acc[:])
-        empty(2, left, acc[:])
-        negate(0)
-        put_difference(0)
-        acc = bank(2, S // 2)
-        project(2, right, acc[:])
-        empty(2, right, acc[:])
-        fetch(1, high)
-        put_sum(1, high)
-        fetch(2, whole)
-        put_sum(2, whole)
-        acc = bank(3, S)
-        project(3, slice(0, S), acc[:])
-        empty(3, slice(0, S), acc[:])
-        fetch(3, whole)
-        negate(1)
-        put_difference(1)
-        put_sum(3, whole)
-        negate(2)
-        put_difference(2)
+            project(0, slice(c * CHUNK, (c + 1) * CHUNK), c, False)
+        project(1, left, 4, True)
+        project(1, right, 5, True)
+        move(a[0][:], y[0][:].indirect(la_sb[:]), True)
+        move(b[0][:], y[0][:].indirect(lb_sb[:]), False)
+        project(2, slice(0, S), 6, False)
+        project(3, left, 7, True)
+        project(3, right, 0, False)
+        move(a[1][:], y[1][:].indirect(la_sb[:]), False)
+        move(b[1][:], y[1][:].indirect(lb_sb[:]), True)
+        move(a[2][:], y[2][:].indirect(la_sb[:]), True)
+        move(b[2][:], y[2][:].indirect(lb_sb[:]), False)
+        move(a[3][:], y[3][:].indirect(la_sb[:]), True)
 
-        z_grouped = tile("z_grouped", [P, S, PACK], BF16, tag="y2")
-        for half in (left, right):
-            regroup(nc.scalar.copy, 0, half)
-        negate(PACK - 1)
-        put_difference(PACK - 1)
-        w2_codes = tile("w2_codes", [P, N], U32, tag="y1")
+        def combine(t, out, op):
+            nc.gpsimd.tensor_tensor(out[t][:], a[t][:], b[t][:], op)
+
+        def put(t, values, lists):
+            move(z[t][:].indirect(lists[:]), values[t][:], t in (1, 2))
+
+        combine(0, df, SUB)
+        for t in range(PACK - 1):
+            combine(t, sm, ADD)
+            put(t, sm, la_sb)
+        b.append(tile("b3", [P, V], F32, tag="b0"))
+        move(b[3][:], y[3][:].indirect(lb_sb[:]), False)
+        put(0, df, lb_sb)
+        df[1] = tile("df1", [P, V], F32, tag="y2")
+        for t in (1, 2):
+            combine(t, df, SUB)
+            put(t, df, lb_sb)
+        combine(3, sm, ADD)
+        put(3, sm, la_sb)
+        combine(3, df, SUB)
+        put(3, df, lb_sb)
+
+        halves = (left, right)
+        z_pairs = [tile("z_pairs%d" % h, [P, 2, S // 2, 2], BF16, tag=("a3", "a2")[h]) for h in range(2)]
+        for t in range(2):
+            for h in range(2):
+                nc.gpsimd.tensor_scalar(z_pairs[h][:, 0, :, t], z[t][:, halves[h]], 1.0, 0.0, MULT, ADD)
+        for h in range(2):
+            nc.vector.tensor_copy(out=z_pairs[h][:, 1, :, 0], in_=z[2][:, halves[h]])
+        w2_codes = tile("w2_codes", [P, N], U32, tag="df3")
         nc.scalar.copy(
             out=w2_codes[:].rearrange("p (t g i) -> p g t i", t=PACK, i=LINE),
             in_=w2_word_raw[:].rearrange("p (g i t) -> p g t i", t=PACK, i=LINE),
         )
-        for slot in (1, 2):
-            for half in (left, right):
-                regroup(nc.scalar.copy, slot, half)
-        for c in range(CHUNKS):
-            regroup(nc.vector.tensor_copy if c < 2 else nc.scalar.copy, PACK - 1, slice(c * CHUNK, (c + 1) * CHUNK))
+        z_grouped = tiles("z_grouped", CHUNKS, [P, CHUNK, PACK], BF16)
+        for h in range(2):
+            for k in range(2):
+                cols = slice(k * CHUNK, (k + 1) * CHUNK)
+                nc.vector.tensor_copy(out=z_pairs[h][:, 1, cols, 1], in_=z[3][:, halves[h]][:, cols])
+            for k in range(2):
+                cols = slice(k * CHUNK, (k + 1) * CHUNK)
+                nc.vector.tensor_copy(
+                    out=z_grouped[2 * h + k][:].bitcast(I32),
+                    in_=z_pairs[h][:].rearrange("p u c e -> p u (c e)").bitcast(I32)[:, :, cols].rearrange("p u c -> p c u"),
+                )
 
         chunk_cols = [slice(c * CHUNK, (c + 1) * CHUNK) for c in range(CHUNKS)]
-        halves = (left, right)
         z_codes = tiles("z_codes", CHUNKS, [P, CHUNK], U32)
         z_scale = tiles("z_scale", CHUNKS, [P, CHUNK], U8)
         result = tiles("result", 2, [P, PACK, S // 2], F32)
@@ -216,12 +203,12 @@ def tile_picked_haarinp_none_po_kernel(tc, x_words, x_scales, w1, w2_words, w2_s
         out_words = out_1[0].rearrange("p n t -> p (n t)").bitcast(I32)
 
         for c in range(CHUNKS):
-            quantize(nc, z_codes[c][:], z_scale[c][:], z_grouped[:, chunk_cols[c], :])
+            quantize(nc, z_codes[c][:], z_scale[c][:], z_grouped[c][:])
         for h in range(2):
             for first in range(0, PACK, 2):
                 for k in range(2):
                     c = 2 * h + k
-                    acc = psum.tile([P, 2, CHUNK], F32, name="acc", tag="bank%d" % ((6 + 4 * h + first + k) % 8))
+                    acc = psum.tile([P, 2, CHUNK], F32, name="acc", tag="bank%d" % (4 * h + first + k))
                     for t in range(first, first + 2):
                         w_cols = slice(t * P, (t + 1) * P)
                         product(nc, acc[:, t - first, :], w2_codes[:, w_cols], w2_scale[:, w_cols], z_codes[c][:], z_scale[c][:])

@@ -46,6 +46,7 @@ def tile_picked_haarinp_none_po_kernel(tc, x_words, x_scales, w1, w2_words, w2_s
     nc = tc.nc
     with ExitStack() as ctx:
         keep = ctx.enter_context(tc.tile_pool(name="keep", bufs=1))
+        shared = ctx.enter_context(tc.tile_pool(name="shared", bufs=1))
         psum = ctx.enter_context(tc.psum_pool(name="psum", bufs=1))
 
         def tile(name, shape, dtype, tag=None):
@@ -109,12 +110,13 @@ def tile_picked_haarinp_none_po_kernel(tc, x_words, x_scales, w1, w2_words, w2_s
         for t in range(PACK):
             quantize(nc, w1_codes[t][:], w1_scale[t][:], w1_grouped[t // 2][:, t % 2])
 
-        y = tiles("y", PACK, [P, S], F32)
+        y = [shared.tile([P, S], F32, name="y1", offset=6144) if t == 1 else tile("y%d" % t, [P, S], F32) for t in range(PACK)]
         a = tiles("a", PACK, [P, V], F32)
         b = tiles("b", PACK - 1, [P, V], F32)
-        sm = tiles("sm", PACK, [P, V], F32)
-        df = {t: tile("df%d" % t, [P, V], F32) for t in (0, 2, 3)}
-        z = tiles("z", PACK, [P, S], F32)
+        sm = tiles("sm", PACK - 1, [P, V], F32) + [shared.tile([P, V], F32, name="sm3", offset=1536)]
+        df = {3: tile("df3", [P, V], F32)}
+        df[0] = shared.tile([P, V], F32, name="df0", offset=7168)
+        z = [shared.tile([P, S], F32, name="z0", offset=5120)] + [tile("z%d" % t, [P, S], F32) for t in range(1, PACK)]
         left, right = slice(0, S // 2), slice(S // 2, S)
 
         def project(t, cols, bank, on_vector):
@@ -139,9 +141,9 @@ def tile_picked_haarinp_none_po_kernel(tc, x_words, x_scales, w1, w2_words, w2_s
         move(b[0][:], y[0][:].indirect(lb_sb[:]), False)
         project(2, slice(0, S), 6, False)
         project(3, left, 7, True)
-        project(3, right, 0, False)
         move(a[1][:], y[1][:].indirect(la_sb[:]), False)
         move(b[1][:], y[1][:].indirect(lb_sb[:]), True)
+        project(3, right, 0, True)
         move(a[2][:], y[2][:].indirect(la_sb[:]), True)
         move(b[2][:], y[2][:].indirect(lb_sb[:]), False)
         move(a[3][:], y[3][:].indirect(la_sb[:]), True)
@@ -152,45 +154,46 @@ def tile_picked_haarinp_none_po_kernel(tc, x_words, x_scales, w1, w2_words, w2_s
         def put(t, values, lists):
             move(z[t][:].indirect(lists[:]), values[t][:], t in (1, 2))
 
-        combine(0, df, SUB)
-        for t in range(PACK - 1):
+        for t in range(2):
             combine(t, sm, ADD)
             put(t, sm, la_sb)
+        combine(0, df, SUB)
         b.append(tile("b3", [P, V], F32, tag="b0"))
         move(b[3][:], y[3][:].indirect(lb_sb[:]), False)
         put(0, df, lb_sb)
+        combine(2, sm, ADD)
+        put(2, sm, la_sb)
         df[1] = tile("df1", [P, V], F32, tag="y2")
-        for t in (1, 2):
-            combine(t, df, SUB)
-            put(t, df, lb_sb)
+        combine(1, df, SUB)
+        put(1, df, lb_sb)
         combine(3, sm, ADD)
         put(3, sm, la_sb)
-        combine(3, df, SUB)
-        put(3, df, lb_sb)
+        df[2] = tile("df2", [P, V], F32, tag="y3")
+        for t in (2, 3):
+            combine(t, df, SUB)
+            put(t, df, lb_sb)
 
         halves = (left, right)
-        z_pairs = [tile("z_pairs%d" % h, [P, 2, S // 2, 2], BF16, tag=("a3", "a2")[h]) for h in range(2)]
-        for t in range(2):
-            for h in range(2):
-                nc.gpsimd.tensor_scalar(z_pairs[h][:, 0, :, t], z[t][:, halves[h]], 1.0, 0.0, MULT, ADD)
+        z_pairs = [tile("z_pairs0", [P, 2, S // 2, 2], BF16, tag="a3"), shared.tile([P, 2, S // 2, 2], BF16, name="z_pairs1", offset=0)]
         for h in range(2):
-            nc.vector.tensor_copy(out=z_pairs[h][:, 1, :, 0], in_=z[2][:, halves[h]])
-        w2_codes = tile("w2_codes", [P, N], U32, tag="df3")
+            for t in range(2):
+                nc.gpsimd.tensor_scalar(z_pairs[h][:, 0, :, t], z[t][:, halves[h]], 1.0, 0.0, MULT, ADD)
+        nc.vector.tensor_copy(out=z_pairs[0][:, 1, :, 0], in_=z[2][:, left])
+        w2_codes = shared.tile([P, N], U32, name="w2_codes", offset=2048, align_bytes=64)
         nc.scalar.copy(
             out=w2_codes[:].rearrange("p (t g i) -> p g t i", t=PACK, i=LINE),
             in_=w2_word_raw[:].rearrange("p (g i t) -> p g t i", t=PACK, i=LINE),
         )
+        for e in range(2):
+            nc.scalar.copy(out=z_pairs[1][:, 1, :, e], in_=z[2 + e][:, right])
         z_grouped = tiles("z_grouped", CHUNKS, [P, CHUNK, PACK], BF16)
-        for h in range(2):
-            for k in range(2):
-                cols = slice(k * CHUNK, (k + 1) * CHUNK)
-                nc.vector.tensor_copy(out=z_pairs[h][:, 1, cols, 1], in_=z[3][:, halves[h]][:, cols])
-            for k in range(2):
-                cols = slice(k * CHUNK, (k + 1) * CHUNK)
-                nc.vector.tensor_copy(
-                    out=z_grouped[2 * h + k][:].bitcast(I32),
-                    in_=z_pairs[h][:].rearrange("p u c e -> p u (c e)").bitcast(I32)[:, :, cols].rearrange("p u c -> p c u"),
-                )
+        for k in range(2):
+            cols = slice(k * CHUNK, (k + 1) * CHUNK)
+            nc.vector.tensor_copy(out=z_pairs[0][:, 1, cols, 1], in_=z[3][:, cols])
+        for c in range(CHUNKS):
+            words = z_pairs[c // 2][:].rearrange("p u c e -> p u (c e)").bitcast(I32)
+            cols = slice(c % 2 * CHUNK, (c % 2 + 1) * CHUNK)
+            nc.vector.tensor_copy(out=z_grouped[c][:].bitcast(I32), in_=words[:, :, cols].rearrange("p u c -> p c u"))
 
         chunk_cols = [slice(c * CHUNK, (c + 1) * CHUNK) for c in range(CHUNKS)]
         z_codes = tiles("z_codes", CHUNKS, [P, CHUNK], U32)

@@ -50,7 +50,7 @@ def tile_picked_haarinp_none_po_kernel(tc, x_words, x_scales, w1, w2_words, w2_s
         psum = ctx.enter_context(tc.psum_pool(name="psum", bufs=1))
 
         def tile(name, shape, dtype, tag=None):
-            return keep.tile(shape, dtype, name=name, tag=tag or name, align_bytes=64)
+            return keep.tile(shape, dtype, name=name, tag=tag or name, align_bytes=256)
 
         def tiles(name, count, shape, dtype):
             return [tile("%s%d" % (name, i), shape, dtype) for i in range(count)]

@@ -169,7 +169,7 @@ def tile_picked_haarinp_none_po_kernel(tc, x_words, x_scales, w1, w2_words, w2_s
         combine(3, sm, ADD)
         put(3, sm, la_sb)
         df[2] = tile("df2", [P, V], F32, tag="y3")
-        for t in (2, 3):
+        for t in (3, 2):
             combine(t, df, SUB)
             put(t, df, lb_sb)
 
@@ -179,13 +179,14 @@ def tile_picked_haarinp_none_po_kernel(tc, x_words, x_scales, w1, w2_words, w2_s
             for t in range(2):
                 nc.gpsimd.tensor_scalar(z_pairs[h][:, 0, :, t], z[t][:, halves[h]], 1.0, 0.0, MULT, ADD)
         nc.vector.tensor_copy(out=z_pairs[0][:, 1, :, 0], in_=z[2][:, left])
-        w2_codes = shared.tile([P, N], U32, name="w2_codes", offset=2048, align_bytes=64)
-        nc.scalar.copy(
-            out=w2_codes[:].rearrange("p (t g i) -> p g t i", t=PACK, i=LINE),
-            in_=w2_word_raw[:].rearrange("p (g i t) -> p g t i", t=PACK, i=LINE),
-        )
-        for e in range(2):
-            nc.scalar.copy(out=z_pairs[1][:, 1, :, e], in_=z[2 + e][:, right])
+        w2_planes = w2_word_raw[:].rearrange("p (g i t) -> p g t i", t=PACK, i=LINE)
+        w2_first = shared.tile([P, P], U32, name="w2_first", offset=2048, align_bytes=64)
+        nc.scalar.copy(out=w2_first[:].rearrange("p (g i) -> p g i", i=LINE), in_=w2_planes[:, :, 0, :])
+        nc.scalar.copy(out=z_pairs[1][:, 1, :, 0], in_=z[2][:, right])
+        w2_rest = tile("w2_rest", [P, PACK - 1, P], U32, tag="df3")
+        nc.scalar.copy(out=w2_rest[:].rearrange("p t (g i) -> p g t i", i=LINE), in_=w2_planes[:, :, 1:, :])
+        w2_codes = [w2_first[:]] + [w2_rest[:, t, :] for t in range(PACK - 1)]
+        nc.scalar.copy(out=z_pairs[1][:, 1, :, 1], in_=z[3][:, right])
         z_grouped = tiles("z_grouped", CHUNKS, [P, CHUNK, PACK], BF16)
         for k in range(2):
             cols = slice(k * CHUNK, (k + 1) * CHUNK)
@@ -214,7 +215,7 @@ def tile_picked_haarinp_none_po_kernel(tc, x_words, x_scales, w1, w2_words, w2_s
                     acc = psum.tile([P, 2, CHUNK], F32, name="acc", tag="bank%d" % (4 * h + first + k))
                     for t in range(first, first + 2):
                         w_cols = slice(t * P, (t + 1) * P)
-                        product(nc, acc[:, t - first, :], w2_codes[:, w_cols], w2_scale[:, w_cols], z_codes[c][:], z_scale[c][:])
+                        product(nc, acc[:, t - first, :], w2_codes[t], w2_scale[:, w_cols], z_codes[c][:], z_scale[c][:])
                     nc.scalar.copy(out=result[h][:, first : first + 2, chunk_cols[k]], in_=acc[:])
                     if first > 0:
                         nc.vector.tensor_copy(

@@ -23,6 +23,7 @@ CHUNK = 128
 CHUNKS = S // CHUNK
 LINE = 4
 LIST = 16
+WARM_UPS = 3
 
 FLOPS = 2 * K * H * S + 2 * H * N * S
 
@@ -186,6 +187,9 @@ def tile_picked_haarinp_none_po_kernel(tc, x_words, x_scales, w1, w2_words, w2_s
         w2_rest = tile("w2_rest", [P, PACK - 1, P], U32, tag="df3")
         nc.scalar.copy(out=w2_rest[:].rearrange("p t (g i) -> p g t i", i=LINE), in_=w2_planes[:, :, 1:, :])
         w2_codes = [w2_first[:]] + [w2_rest[:, t, :] for t in range(PACK - 1)]
+        idle = psum.tile([P, WARM_UPS, P], F32, name="idle", tag="bank7")
+        for t in range(WARM_UPS):
+            product(nc, idle[:, t, :], w2_codes[1], w2_scale[:, P : 2 * P], w1_codes[t][:], w1_scale[t][:])
         nc.scalar.copy(out=z_pairs[1][:, 1, :, 1], in_=z[3][:, right])
         z_grouped = tiles("z_grouped", CHUNKS, [P, CHUNK, PACK], BF16)
         for k in range(2):

@@ -114,7 +114,7 @@ def tile_picked_haarinp_none_po_kernel(tc, x_words, x_scales, w1, w2_words, w2_s
         y = [shared.tile([P, S], F32, name="y1", offset=6144) if t == 1 else tile("y%d" % t, [P, S], F32) for t in range(PACK)]
         a = tiles("a", PACK, [P, V], F32)
         b = tiles("b", PACK - 1, [P, V], F32)
-        sm = tiles("sm", PACK - 1, [P, V], F32) + [shared.tile([P, V], F32, name="sm3", offset=1536)]
+        sm = tiles("sm", PACK, [P, V], F32)
         df = {3: tile("df3", [P, V], F32)}
         df[0] = shared.tile([P, V], F32, name="df0", offset=7168)
         z = [shared.tile([P, S], F32, name="z0", offset=5120)] + [tile("z%d" % t, [P, S], F32) for t in range(1, PACK)]
@@ -175,13 +175,13 @@ def tile_picked_haarinp_none_po_kernel(tc, x_words, x_scales, w1, w2_words, w2_s
             put(t, df, lb_sb)
 
         halves = (left, right)
-        z_pairs = [tile("z_pairs0", [P, 2, S // 2, 2], BF16, tag="a3"), shared.tile([P, 2, S // 2, 2], BF16, name="z_pairs1", offset=0)]
-        for h in range(2):
-            for t in range(2):
+        z_pairs = [tile("z_pairs%d" % h, [P, 2, S // 2, 2], BF16, tag=("a3", "b0")[h]) for h in range(2)]
+        for t in range(2):
+            for h in range(2):
                 nc.gpsimd.tensor_scalar(z_pairs[h][:, 0, :, t], z[t][:, halves[h]], 1.0, 0.0, MULT, ADD)
         nc.vector.tensor_copy(out=z_pairs[0][:, 1, :, 0], in_=z[2][:, left])
         w2_planes = w2_word_raw[:].rearrange("p (g i t) -> p g t i", t=PACK, i=LINE)
-        w2_first = shared.tile([P, P], U32, name="w2_first", offset=2048, align_bytes=64)
+        w2_first = tile("w2_first", [P, P], U32, tag="sm3")
         nc.scalar.copy(out=w2_first[:].rearrange("p (g i) -> p g i", i=LINE), in_=w2_planes[:, :, 0, :])
         nc.scalar.copy(out=z_pairs[1][:, 1, :, 0], in_=z[2][:, right])
         w2_rest = tile("w2_rest", [P, PACK - 1, P], U32, tag="df3")
@@ -200,11 +200,9 @@ def tile_picked_haarinp_none_po_kernel(tc, x_words, x_scales, w1, w2_words, w2_s
             cols = slice(c % 2 * CHUNK, (c % 2 + 1) * CHUNK)
             nc.vector.tensor_copy(out=z_grouped[c][:].bitcast(I32), in_=words[:, :, cols].rearrange("p u c -> p c u"))
 
-        chunk_cols = [slice(c * CHUNK, (c + 1) * CHUNK) for c in range(CHUNKS)]
         z_codes = tiles("z_codes", CHUNKS, [P, CHUNK], U32)
         z_scale = tiles("z_scale", CHUNKS, [P, CHUNK], U8)
         result = tiles("result", 2, [P, PACK, S // 2], F32)
-        result_grouped = tiles("result_grouped", CHUNKS, [P, CHUNK, PACK], BF16)
         out_codes = tile("out_codes", [P, S], U32)
         out_scale = tile("out_scale", [P, S], U8)
         out_rows = out_0.rearrange("(p t) n -> p t n", t=PACK)
@@ -212,21 +210,28 @@ def tile_picked_haarinp_none_po_kernel(tc, x_words, x_scales, w1, w2_words, w2_s
 
         for c in range(CHUNKS):
             quantize(nc, z_codes[c][:], z_scale[c][:], z_grouped[c][:])
+        banks = ["bank%d" % (i % 8) for i in range(9)]
         for h in range(2):
             for first in range(0, PACK, 2):
-                for k in range(2):
-                    c = 2 * h + k
-                    acc = psum.tile([P, 2, CHUNK], F32, name="acc", tag="bank%d" % (4 * h + first + k))
+                last = h == 1 and first > 0
+                spans = ((0, CHUNK), (CHUNK, CHUNK // 2), (3 * CHUNK // 2, CHUNK // 2)) if last else ((0, CHUNK), (CHUNK, CHUNK))
+                for at, width in spans:
+                    c = 2 * h + at // CHUNK
+                    inner = slice(at % CHUNK, at % CHUNK + width)
+                    cols = slice(at, at + width)
+                    whole = slice(h * S // 2 + at, h * S // 2 + at + width)
+                    acc = psum.tile([P, 2, width], F32, name="acc", tag=banks.pop(0))
                     for t in range(first, first + 2):
                         w_cols = slice(t * P, (t + 1) * P)
-                        product(nc, acc[:, t - first, :], w2_codes[t], w2_scale[:, w_cols], z_codes[c][:], z_scale[c][:])
-                    nc.scalar.copy(out=result[h][:, first : first + 2, chunk_cols[k]], in_=acc[:])
+                        product(nc, acc[:, t - first, :], w2_codes[t], w2_scale[:, w_cols], z_codes[c][:, inner], z_scale[c][:, inner])
+                    nc.scalar.copy(out=result[h][:, first : first + 2, cols], in_=acc[:])
                     if first > 0:
+                        grouped = tile("result_grouped%d" % whole.start, [P, width, PACK], BF16)
                         nc.vector.tensor_copy(
-                            out=result_grouped[c][:].rearrange("p (g i) t -> p g t i", i=LINE),
-                            in_=result[h][:, :, chunk_cols[k]].rearrange("p t (g i) -> p g t i", i=LINE),
+                            out=grouped[:].rearrange("p (g i) t -> p g t i", i=LINE),
+                            in_=result[h][:, :, cols].rearrange("p t (g i) -> p g t i", i=LINE),
                         )
-                        quantize(nc, out_codes[:, chunk_cols[c]], out_scale[:, chunk_cols[c]], result_grouped[c][:])
+                        quantize(nc, out_codes[:, whole], out_scale[:, whole], grouped[:])
                 nc.sync.dma_start(out=out_rows[:, first : first + 2, halves[h]], in_=result[h][:, first : first + 2, :])
         nc.sync.dma_start(out=out_words, in_=out_codes[:].bitcast(I32))
         for q in range(QUADS):

@@ -143,8 +143,9 @@ def tile_picked_haarinp_none_po_kernel(tc, x_words, x_scales, w1, w2_words, w2_s
         project(2, slice(0, S), 6, False)
         project(3, left, 7, True)
         move(a[1][:], y[1][:].indirect(la_sb[:]), False)
+        project(3, slice(3 * CHUNK, S), 1, False)
         move(b[1][:], y[1][:].indirect(lb_sb[:]), True)
-        project(3, right, 0, True)
+        project(3, slice(2 * CHUNK, 3 * CHUNK), 0, True)
         move(a[2][:], y[2][:].indirect(la_sb[:]), True)
         move(b[2][:], y[2][:].indirect(lb_sb[:]), False)
         move(a[3][:], y[3][:].indirect(la_sb[:]), True)

from contextlib import ExitStack

import concourse.mybir as mybir

K, T, S, V, N, H = 512, 2048, 512, 256, 512, 512

F32 = mybir.dt.float32
BF16 = mybir.dt.bfloat16
I32 = mybir.dt.int32
U32 = mybir.dt.uint32
U16 = mybir.dt.uint16
U8 = mybir.dt.uint8
FP8X4 = mybir.dt.float8_e4m3fn_x4
COPY = mybir.ActivationFunctionType.Copy
ADD = mybir.AluOpType.add
SUB = mybir.AluOpType.subtract
MULT = mybir.AluOpType.mult

P = 128
PACK = 4
QUADS = 4
CHUNK = 128
CHUNKS = S // CHUNK
LINE = 4
LIST = 16
WARM_UPS = 3

FLOPS = 2 * K * H * S + 2 * H * N * S


def quantize(nc, codes, scale, values):
    nc.vector.quantize_mx(out=codes.bitcast(FP8X4), scales=scale, in_=values.rearrange("p n t -> p (n t)"))


def product(nc, acc, w_codes, w_scale, codes, scale):
    nc.tensor.matmul_mx(
        out=acc, lhsT=w_codes.bitcast(FP8X4), lhsT_scale=w_scale, rhs=codes.bitcast(FP8X4), rhs_scale=scale, start=True, stop=True
    )


def move_scale_rows(nc, plane, rows, first):
    for q in range(QUADS):
        nc.sync.dma_start(out=plane[32 * q : 32 * q + 4, :].bitcast(I32), in_=rows[first + 4 * q : first + 4 * q + 4, :].bitcast(I32))


def tile_picked_haarinp_none_po_kernel(tc, x_words, x_scales, w1, w2_words, w2_scales, offs, la, lb, out_0, out_1, out_2):
    nc = tc.nc
    with ExitStack() as ctx:
        keep = ctx.enter_context(tc.tile_pool(name="keep", bufs=1))
        shared = ctx.enter_context(tc.tile_pool(name="shared", bufs=1))
        psum = ctx.enter_context(tc.psum_pool(name="psum", bufs=1))

        def tile(name, shape, dtype, tag=None):
            return keep.tile(shape, dtype, name=name, tag=tag or name, align_bytes=256)

        def tiles(name, count, shape, dtype):
            return [tile("%s%d" % (name, i), shape, dtype) for i in range(count)]

        offs_sb = keep.tile([P, S // LIST], U16, name="offs_sb")
        la_sb = keep.tile([P, V // LIST], U16, name="la_sb")
        lb_sb = keep.tile([P, V // LIST], U16, name="lb_sb")
        x_word_table = tile("x_word_table", [P, T], U32)
        x_scale_table = tile("x_scale_table", [P, T], U8, tag="x_scale_table")
        x_word_picked = tile("x_word_picked", [P, S], U32)
        x_scale_gathered = tile("x_scale_gathered", [P, S], U8)
        x_scale_picked = tile("x_scale_picked", [P, S], U8)
        w1_early = tile("w1_early", [P, PACK - 1, H], F32)
        w1_late = tile("w1_late", [P, H], F32)
        w2_scale_raw = tile("w2_scale_raw", [P, N], U8)
        w2_scale_dealt = tile("w2_scale_dealt", [P, N], U8)
        w2_scale = tile("w2_scale", [P, N], U8)

        for first, stop in ((0, 16), (32, 64), (64, P)):
            nc.vector.memset(x_scale_table[first:stop, :].bitcast(I32), 0)
        nc.vector.memset(w2_scale_raw[:].bitcast(I32), 0)
        nc.vector.memset(x_scale_picked[:].bitcast(I32), 0)
        nc.vector.memset(w2_scale[:].bitcast(I32), 0)

        w1_rows = w1.rearrange("(p j) c -> p j c", j=PACK)
        nc.scalar.dma_start(out=x_scale_table[16:32, :].bitcast(I32), in_=x_scales[0].bitcast(I32))
        nc.sync.dma_start(offs_sb[:], offs)
        nc.sync.dma_start(out=x_word_table[:].bitcast(I32), in_=x_words[0].rearrange("p n t -> p (n t)").bitcast(I32))
        nc.sync.dma_start(out=w2_scale_raw[0:16, :].bitcast(I32), in_=w2_scales[0].bitcast(I32))
        nc.sync.dma_start(out=w1_early[:], in_=w1_rows[:, : PACK - 1, :])
        nc.sync.dma_start(out=w1_late[:], in_=w1_rows[:, PACK - 1, :])
        nc.sync.dma_start(la_sb[:], la)
        nc.sync.dma_start(lb_sb[:], lb)

        nc.vector.tensor_copy(out=x_scale_gathered[:], in_=x_scale_table[:].indirect(offs_sb[:]))
        move_scale_rows(nc, x_scale_picked, x_scale_gathered, 16)
        w2_word_raw = tile("w2_word_raw", [P, N], U32, tag="x_scale_table")
        nc.sync.dma_start(out=w2_word_raw[:].bitcast(I32), in_=w2_words[0].rearrange("p n t -> p (n t)").bitcast(I32))
        nc.vector.tensor_copy(out=x_word_picked[:], in_=x_word_table[:].indirect(offs_sb[:]))
        nc.vector.tensor_copy(
            out=w2_scale_dealt[:].rearrange("p (t g i) -> p g t i", t=PACK, i=16),
            in_=w2_scale_raw[:].rearrange("p (g i t) -> p g t i", t=PACK, i=16),
        )
        move_scale_rows(nc, w2_scale, w2_scale_dealt, 0)

        w1_grouped = tiles("w1_grouped", 2, [P, 2, P, PACK], BF16)
        w1_codes = tiles("w1_codes", PACK, [P, P], U32)
        w1_scale = tiles("w1_scale", PACK, [P, P], U8)
        early = w1_early[:].rearrange("p j (m u e) -> p u m j e", e=2, u=2)
        late = w1_late[:].rearrange("p (m u e) -> p u m e", e=2, u=2)
        nc.vector.tensor_copy(out=w1_grouped[0][:, :, :, : PACK - 1].rearrange("p e m j -> p m j e"), in_=early[:, 0])
        nc.scalar.copy(out=w1_grouped[1][:, :, :, : PACK - 1].rearrange("p e m j -> p m j e"), in_=early[:, 1])
        for e in range(2):
            nc.vector.tensor_copy(out=w1_grouped[0][:, e, :, PACK - 1], in_=late[:, 0, :, e])
        nc.scalar.copy(out=w1_grouped[1][:, :, :, PACK - 1].rearrange("p e m -> p m e"), in_=late[:, 1])

        for t in range(PACK):
            quantize(nc, w1_codes[t][:], w1_scale[t][:], w1_grouped[t // 2][:, t % 2])

        y = [shared.tile([P, S], F32, name="y1", offset=6144) if t == 1 else tile("y%d" % t, [P, S], F32) for t in range(PACK)]
        a = tiles("a", PACK, [P, V], F32)
        b = tiles("b", PACK - 1, [P, V], F32)
        sm = tiles("sm", PACK, [P, V], F32)
        df = {3: tile("df3", [P, V], F32)}
        df[0] = shared.tile([P, V], F32, name="df0", offset=7168)
        z = [shared.tile([P, S], F32, name="z0", offset=5120)] + [tile("z%d" % t, [P, S], F32) for t in range(1, PACK)]
        left, right = slice(0, S // 2), slice(S // 2, S)

        def project(t, cols, bank, on_vector):
            acc = psum.tile([P, cols.stop - cols.start], F32, name="acc", tag="bank%d" % bank)
            product(nc, acc[:], w1_codes[t][:], w1_scale[t][:], x_word_picked[:, cols], x_scale_picked[:, cols])
            if on_vector:
                nc.vector.tensor_scalar_mul(y[t][:, cols], acc[:], 0.75)
            else:
                nc.scalar.activation(out=y[t][:, cols], in_=acc[:], func=COPY, scale=0.75)

        def move(out, in_, on_vector):
            if on_vector:
                nc.vector.tensor_copy(out=out, in_=in_)
            else:
                nc.scalar.activation(out=out, in_=in_, func=COPY)

        for c in range(CHUNKS):
            project(0, slice(c * CHUNK, (c + 1) * CHUNK), c, False)
        project(1, left, 4, True)
        project(1, right, 5, True)
        move(a[0][:], y[0][:].indirect(la_sb[:]), True)
        move(b[0][:], y[0][:].indirect(lb_sb[:]), False)
        project(2, slice(0, S), 6, False)
        project(3, left, 7, True)
        move(a[1][:], y[1][:].indirect(la_sb[:]), False)
        project(3, slice(3 * CHUNK, S), 1, False)
        move(b[1][:], y[1][:].indirect(lb_sb[:]), True)
        project(3, slice(2 * CHUNK, 3 * CHUNK), 0, True)
        move(a[2][:], y[2][:].indirect(la_sb[:]), True)
        move(b[2][:], y[2][:].indirect(lb_sb[:]), False)
        move(a[3][:], y[3][:].indirect(la_sb[:]), True)

        def combine(t, out, op):
            nc.gpsimd.tensor_tensor(out[t][:], a[t][:], b[t][:], op)

        def put(t, values, lists):
            move(z[t][:].indirect(lists[:]), values[t][:], t in (1, 2))

        for t in range(2):
            combine(t, sm, ADD)
            put(t, sm, la_sb)
        combine(0, df, SUB)
        b.append(tile("b3", [P, V], F32, tag="b0"))
        move(b[3][:], y[3][:].indirect(lb_sb[:]), False)
        put(0, df, lb_sb)
        combine(2, sm, ADD)
        put(2, sm, la_sb)
        df[1] = tile("df1", [P, V], F32, tag="y2")
        combine(1, df, SUB)
        put(1, df, lb_sb)
        combine(3, sm, ADD)
        put(3, sm, la_sb)
        df[2] = tile("df2", [P, V], F32, tag="y3")
        for t in (3, 2):
            combine(t, df, SUB)
            put(t, df, lb_sb)

        halves = (left, right)
        z_pairs = [tile("z_pairs%d" % h, [P, 2, S // 2, 2], BF16, tag=("a3", "b0")[h]) for h in range(2)]
        for t in range(2):
            for h in range(2):
                nc.gpsimd.tensor_scalar(z_pairs[h][:, 0, :, t], z[t][:, halves[h]], 1.0, 0.0, MULT, ADD)
        nc.vector.tensor_copy(out=z_pairs[0][:, 1, :, 0], in_=z[2][:, left])
        w2_planes = w2_word_raw[:].rearrange("p (g i t) -> p g t i", t=PACK, i=LINE)
        w2_first = tile("w2_first", [P, P], U32, tag="sm3")
        nc.scalar.copy(out=w2_first[:].rearrange("p (g i) -> p g i", i=LINE), in_=w2_planes[:, :, 0, :])
        nc.scalar.copy(out=z_pairs[1][:, 1, :, 0], in_=z[2][:, right])
        w2_rest = tile("w2_rest", [P, PACK - 1, P], U32, tag="df3")
        nc.scalar.copy(out=w2_rest[:].rearrange("p t (g i) -> p g t i", i=LINE), in_=w2_planes[:, :, 1:, :])
        w2_codes = [w2_first[:]] + [w2_rest[:, t, :] for t in range(PACK - 1)]
        idle = psum.tile([P, WARM_UPS, P], F32, name="idle", tag="bank7")
        for t in range(WARM_UPS):
            product(nc, idle[:, t, :], w2_codes[1], w2_scale[:, P : 2 * P], w1_codes[t][:], w1_scale[t][:])
        nc.scalar.copy(out=z_pairs[1][:, 1, :, 1], in_=z[3][:, right])
        z_grouped = tiles("z_grouped", CHUNKS, [P, CHUNK, PACK], BF16)
        for k in range(2):
            cols = slice(k * CHUNK, (k + 1) * CHUNK)
            nc.vector.tensor_copy(out=z_pairs[0][:, 1, cols, 1], in_=z[3][:, cols])
        for c in range(CHUNKS):
            words = z_pairs[c // 2][:].rearrange("p u c e -> p u (c e)").bitcast(I32)
            cols = slice(c % 2 * CHUNK, (c % 2 + 1) * CHUNK)
            nc.vector.tensor_copy(out=z_grouped[c][:].bitcast(I32), in_=words[:, :, cols].rearrange("p u c -> p c u"))

        z_codes = tiles("z_codes", CHUNKS, [P, CHUNK], U32)
        z_scale = tiles("z_scale", CHUNKS, [P, CHUNK], U8)
        result = tiles("result", 2, [P, PACK, S // 2], F32)
        out_codes = tile("out_codes", [P, S], U32)
        out_scale = tile("out_scale", [P, S], U8)
        out_rows = out_0.rearrange("(p t) n -> p t n", t=PACK)
        out_words = out_1[0].rearrange("p n t -> p (n t)").bitcast(I32)

        for c in range(CHUNKS):
            quantize(nc, z_codes[c][:], z_scale[c][:], z_grouped[c][:])
        banks = ["bank%d" % (i % 8) for i in range(9)]
        for h in range(2):
            for first in range(0, PACK, 2):
                last = h == 1 and first > 0
                spans = ((0, CHUNK), (CHUNK, CHUNK // 2), (3 * CHUNK // 2, CHUNK // 2)) if last else ((0, CHUNK), (CHUNK, CHUNK))
                for at, width in spans:
                    c = 2 * h + at // CHUNK
                    inner = slice(at % CHUNK, at % CHUNK + width)
                    cols = slice(at, at + width)
                    whole = slice(h * S // 2 + at, h * S // 2 + at + width)
                    acc = psum.tile([P, 2, width], F32, name="acc", tag=banks.pop(0))
                    for t in range(first, first + 2):
                        w_cols = slice(t * P, (t + 1) * P)
                        product(nc, acc[:, t - first, :], w2_codes[t], w2_scale[:, w_cols], z_codes[c][:, inner], z_scale[c][:, inner])
                    nc.scalar.copy(out=result[h][:, first : first + 2, cols], in_=acc[:])
                    if first > 0:
                        grouped = tile("result_grouped%d" % whole.start, [P, width, PACK], BF16)
                        nc.vector.tensor_copy(
                            out=grouped[:].rearrange("p (g i) t -> p g t i", i=LINE),
                            in_=result[h][:, :, cols].rearrange("p t (g i) -> p g t i", i=LINE),
                        )
                        quantize(nc, out_codes[:, whole], out_scale[:, whole], grouped[:])
                nc.sync.dma_start(out=out_rows[:, first : first + 2, halves[h]], in_=result[h][:, first : first + 2, :])
        nc.sync.dma_start(out=out_words, in_=out_codes[:].bitcast(I32))
        for q in range(QUADS):
            queue = nc.sync if q % 2 == 0 else nc.scalar
            queue.dma_start(out=out_2[0][4 * q : 4 * q + 4, :].bitcast(I32), in_=out_scale[32 * q : 32 * q + 4, :].bitcast(I32))
